import numpy as np
import ml_dtypes


def mxq(x, axis, fmt="e4m3"):
    dtype, down = {"e4m3": (ml_dtypes.float8_e4m3fn, 7), "e5m2": (ml_dtypes.float8_e5m2, 14)}[fmt]
    v = np.moveaxis(np.asarray(x, np.float32).astype(ml_dtypes.bfloat16).astype(np.float64), axis, -1)
    blocks = v.reshape(v.shape[:-1] + (-1, 32))
    amax = np.abs(blocks).max(-1, keepdims=True)
    byte = np.maximum(np.where(amax > 0, np.frexp(amax)[1] - 1 + 127, 0) - down, 1)
    scale = np.exp2(byte - 127.0)
    codes = (blocks / scale).astype(np.float32).astype(dtype).astype(np.float64)
    return np.moveaxis((codes * scale).reshape(v.shape), -1, axis)


WIDE = False


def mx_kscale(k):
    if not WIDE:
        return np.ones(k)
    levels = np.array([10, -10, 5, -5, 0])
    if k % 512:
        return np.exp2(np.random.permutation(np.resize(levels, k // 32))).repeat(32)
    a = np.empty((k // 512, 16))
    for p in range(k // 512):
        a[p, :8] = np.random.permutation(np.resize(levels, 8))
        for g in range(8):
            far = levels[np.abs(levels - a[p, g]) >= 10]
            a[p, g + 8] = far[np.random.randint(len(far))]
    return np.exp2(a.ravel()).repeat(32)


def f64(x):
    return np.asarray(x).astype(np.float64)


def striped(idx):
    return np.tile(idx.reshape(-1, 16).T, (8, 1)).astype(np.uint16)


def unstriped(offs):
    return offs[:16].T.reshape(-1).astype(np.int64)


E2M1 = np.array([0.0, 0.5, 1.0, 1.5, 2.0, 3.0, 4.0, 6.0, -0.0, -0.5, -1.0, -1.5, -2.0, -3.0, -4.0, -6.0])


def pack_weight(w, fmt):
    k, n = w.shape
    w = f64(np.asarray(w, np.float32).astype(ml_dtypes.bfloat16)).reshape(k // 32, 32, n)
    amax = np.abs(w).max(1)
    if fmt == "e4m3":
        byte = np.frexp(amax)[1] - 1 + 127 - 7
    else:
        mant, ex = np.frexp(amax / 6.0)
        byte = np.where(mant > 0.5, ex, ex - 1) + 127
    byte = np.clip(np.where(amax > 0, byte, 1), 1, 254)
    scaled = (w * np.exp2(127.0 - byte)[:, None, :]).reshape(k, n).astype(np.float32)
    by_word = np.ascontiguousarray(scaled.reshape(k // 512, 128, 4, n).transpose(0, 1, 3, 2))
    if fmt == "e4m3":
        words = by_word.astype(ml_dtypes.float8_e4m3fn).view(np.uint8)
    else:
        c = by_word.astype(ml_dtypes.float4_e2m1fn).view(np.uint8) & 0xF
        words = (c[..., 0::2] | (c[..., 1::2] << 4)).reshape(k // 512, 128, 2 * n)
    return np.ascontiguousarray(words), np.ascontiguousarray(byte.astype(np.uint8).reshape(k // 512, 16, n))


def unpack_weight(words, scales, fmt):
    g, _, n = scales.shape
    words = np.ascontiguousarray(words).reshape(g, 128, n, -1)
    if fmt == "e4m3":
        vals = words.view(ml_dtypes.float8_e4m3fn).astype(np.float64)
    else:
        nib = np.empty((g, 128, n, 4), np.uint8)
        nib[..., 0::2] = words & 0xF
        nib[..., 1::2] = words >> 4
        vals = E2M1[nib]
    vals = vals * np.repeat(np.exp2(scales.astype(np.float64) - 127.0), 8, axis=1)[..., None]
    return vals.transpose(0, 1, 3, 2).reshape(g * 512, n)


def gelu(v):
    return 0.5 * v * (1.0 + np.tanh(np.sqrt(2.0 / np.pi) * (v + 0.044715 * v**3)))


K, T, S, H, T2, P, N = 512, 2048, 512, 1024, 2048, 1024, 512

def setup_inputs():
    n = np.random.standard_normal
    s, u = mx_kscale(K)[:, None], mx_kscale(H)[:, None]
    d = {}
    d["tab_words"], d["tab_scales"] = pack_weight(n((K, T)) * s, "e4m3")
    d["offs"] = striped(np.random.permutation(T)[:S])
    prof = np.where(n((K, 1)) > 0, 1.0, -1.0)
    strength = np.random.uniform(-1.0, 1.0, (1, T))
    amp = np.random.uniform(1.6, 2.2, (1, H)) * np.where(n((1, H)) > 0, 1.0, -1.0)
    d["tab2_words"], d["tab2_scales"] = pack_weight((prof * strength + n((K, T))) * s, "e4m3")
    d["offs2"] = striped(np.random.permutation(T)[:S])
    d["w1"] = (1.2 * n((K, H)) / K**0.5 / s).astype(np.float32)
    d["gt"] = (np.exp(0.3 * n(H)) * u[:, 0]).astype(np.float32)
    d["w2_words"], d["w2_scales"] = pack_weight(1.3 * n((H, H)) / H**0.5 / u, "e2m1")
    d["w3_words"], d["w3_scales"] = pack_weight((prof * amp / K + 0.16 * n((K, H)) / K**0.5) / s, "e4m3")
    d["base"] = (0.6 * n((H, S))).astype(np.float32)
    d["page0"] = (0.8 * n((H, T2))).astype(np.float32)
    perm = np.random.permutation(T2)
    d["offs3"] = striped(perm[:S])
    d["offs4"] = striped(perm[S:2 * S])
    d["wg1"] = np.exp(0.3 * n((128, S))).astype(np.float32)
    d["wg2"] = np.exp(0.3 * n((128, S))).astype(np.float32)
    d["offs5"] = striped(np.random.permutation(T2)[:P])
    d["gx"] = (np.exp(0.3 * n(H)) * u[:, 0]).astype(np.float32)
    d["wo"] = (1.2 * n((H, N)) / H**0.5 / u).astype(np.float32)
    return d

def reference(tab_words, tab_scales, offs, tab2_words, tab2_scales, offs2, w1, gt, w2_words, w2_scales, w3_words, w3_scales, base, page0, offs3, offs4, wg1, wg2, offs5, gx, wo):
    v = unpack_weight(tab_words, tab_scales, "e4m3")[:, unstriped(offs)]
    v2 = unpack_weight(tab2_words, tab2_scales, "e4m3")[:, unstriped(offs2)]
    w1q = mxq(f64(w1), 0, "e4m3")
    t = np.tanh(w1q.T @ v) * f64(gt)[:, None]
    h1 = w1q.T @ v + unpack_weight(w2_words, w2_scales, "e2m1").T @ mxq(t, 0, "e4m3")
    h2 = np.sin(unpack_weight(w3_words, w3_scales, "e4m3").T @ v2) + f64(base)
    page = f64(page0).copy()
    page[:, unstriped(offs3)] = np.tile(f64(wg1), (H // 128, 1)) * h1
    page[:, unstriped(offs4)] = np.tile(f64(wg2), (H // 128, 1)) * h2
    x = np.abs(page[:, unstriped(offs5)]) * f64(gx)[:, None]
    return np.tanh(mxq(f64(wo), 0, "e4m3").T @ mxq(x, 0, "e4m3"))

@@ -1,0 +1,337 @@
+import math
+from contextlib import ExitStack
+
+import concourse.mybir as mybir
+from concourse.masks import make_identity
+
+K, T, S, H, T2, PN, N = 512, 2048, 512, 1024, 2048, 1024, 512
+FLOPS = 2 * (3 * K * H * S + H * H * S + H * N * PN)
+
+F32 = mybir.dt.float32
+BF16 = mybir.dt.bfloat16
+I32 = mybir.dt.int32
+U32 = mybir.dt.uint32
+U16 = mybir.dt.uint16
+U8 = mybir.dt.uint8
+FP8X4 = mybir.dt.float8_e4m3fn_x4
+FP4X4 = mybir.dt.float4_e2m1fn_x4
+ACT = mybir.ActivationFunctionType
+ALU = mybir.AluOpType
+
+P = 128
+PACK = 4
+HALF = P * PACK
+HALVES = H // HALF
+TILES = H // P
+QUARTER = PN // 4
+AHEAD = 2
+
+
+def tile_list_embankment_slot_board_kernel(
+    tc, tab_words, tab_scales, offs, tab2_words, tab2_scales, offs2, w1, gt, w2_words, w2_scales,
+    w3_words, w3_scales, base, page0, offs3, offs4, wg1, wg2, offs5, gx, wo, out,
+):
+    nc = tc.nc
+    with ExitStack() as ctx:
+        lists = ctx.enter_context(tc.tile_pool(name="lists", bufs=1))
+        sb = ctx.enter_context(tc.tile_pool(name="sb", bufs=1))
+        psum = ctx.enter_context(tc.psum_pool(name="psum", bufs=1))
+
+        def sbuf(name, shape, dtype, tag=None, bufs=1):
+            return sb.tile(shape, dtype, name=name, tag=tag or name, bufs=bufs, align_bytes=64)
+
+        def bank(name, index):
+            return psum.tile([P, HALF], F32, name=name, tag="bank%d" % index)
+
+        def load_list(name, src):
+            dst = lists.tile(list(src.shape), U16, name=name, tag=name)
+            nc.sync.dma_start(dst[:], src)
+            return dst
+
+        def load_words(name, src, tag):
+            dst = sbuf(name, [P, src.shape[2]], I32, tag=tag, bufs=2)
+            nc.sync.dma_start(dst[:], src[0].rearrange("p n i -> p (n i)").bitcast(I32))
+            return dst
+
+        def zeroed_plane(name, src):
+            dst = sbuf(name, [P, src.shape[0], src.shape[2]], U8)
+            nc.vector.memset(dst[:].bitcast(I32), 0)
+            return dst
+
+        def load_scales(dst, src, queue):
+            words = dst[:].bitcast(I32)
+            rows = src.bitcast(I32).rearrange("a r n -> r a n")
+            for q in range(4):
+                queue.dma_start(words[32 * q : 32 * q + 4, :, :], rows[4 * q : 4 * q + 4, :, :])
+
+        def load_dealt(dst, src, t0, t1):
+            rows = src.rearrange("(p t) j -> p t j", t=PACK)
+            for q in range(4):
+                nc.sync.dma_start(dst[32 * q : 32 * (q + 1), t0:t1, :], rows[:, t0:t1, :])
+
+        def rows_of(src, i):
+            return src.rearrange("(b p t) c -> b t p c", b=HALVES, t=PACK)[i // PACK, i % PACK, :, :]
+
+        def load_page(i):
+            dst = sbuf("page%d" % i, [P, T2], F32)
+            nc.sync.dma_start(dst[:], rows_of(page0, i))
+            return dst
+
+        def load_base(i):
+            dst = sbuf("base%d" % i, [P, S], F32, tag="base", bufs=4)
+            nc.sync.dma_start(dst[:], rows_of(base, i))
+            return dst
+
+        def load_raw(name, src):
+            dst = sbuf(name, [P, PACK, HALF], F32, tag="raw", bufs=2)
+            nc.sync.dma_start(dst[:], src.rearrange("(p j) c -> p j c", j=PACK))
+            return dst
+
+        def load_gain(name, src):
+            dst = sbuf(name, [P, HALVES, PACK], F32)
+            nc.sync.dma_start(dst[:], src.rearrange("(b p t) -> p b t", b=HALVES, t=PACK))
+            return dst
+
+        def woven(name):
+            return sbuf(name, [P, PACK * HALF], BF16, tag="woven", bufs=3)
+
+        def quantize(codes, scales, src):
+            nc.vector.quantize_mx(out=codes.bitcast(FP8X4), scales=scales, in_=src)
+
+        def mx(dst, lhs, lhs_scale, rhs, rhs_scale, start, stop, lhs_dtype=FP8X4):
+            nc.tensor.matmul_mx(
+                out=dst, lhsT=lhs.bitcast(lhs_dtype), lhsT_scale=lhs_scale,
+                rhs=rhs.bitcast(FP8X4), rhs_scale=rhs_scale, start=start, stop=stop,
+            )
+
+        def pick_table(name, words, scales, idx):
+            codes = sbuf(name + "_codes", [P, S], U32)
+            plane = sbuf(name + "_plane", [P, S], U8)
+            nc.vector.tensor_copy(codes[:], words[:].bitcast(U32).indirect(idx[:]))
+            nc.vector.tensor_copy(plane[:], scales[:, 0, :].indirect(idx[:]))
+            return codes, plane
+
+        tab2_sc = zeroed_plane("tab2_sc", tab2_scales)
+        w3_sc = zeroed_plane("w3_sc", w3_scales)
+        tab_sc = zeroed_plane("tab_sc", tab_scales)
+        w2_sc = zeroed_plane("w2_sc", w2_scales)
+        minus_quarter = sbuf("minus_quarter", [P, 1], F32)
+        nc.vector.memset(minus_quarter[:], -0.25)
+        warm = sbuf("warm", [P, 1], F32)
+        nc.scalar.activation(out=warm[:], in_=minus_quarter[:], func=ACT.Silu)
+
+        idx2 = load_list("idx2", offs2)
+        gt_sb = load_gain("gt_sb", gt)
+        gx_sb = load_gain("gx_sb", gx)
+        idx = load_list("idx", offs)
+        idx4 = load_list("idx4", offs4)
+        idx3 = load_list("idx3", offs3)
+        tab2_sb = load_words("tab2_sb", tab2_words, "wide")
+        w3_sb = load_words("w3_sb", w3_words, "codes")
+        load_scales(tab2_sc, tab2_scales, nc.sync)
+        load_scales(w3_sc, w3_scales, nc.gpsimd)
+        tab_sb = load_words("tab_sb", tab_words, "wide")
+        idx5 = load_list("idx5", offs5)
+        load_scales(tab_sc, tab_scales, nc.sync)
+        ident = sbuf("ident", [P, P], F32)
+        make_identity(nc, ident[:])
+        w2_sb = sbuf("w2_sb", [P, HALVES, H // 2], I32, tag="codes", bufs=2)
+        nc.sync.dma_start(w2_sb[:], w2_words.bitcast(I32).rearrange("a p n -> p a n"))
+        load_scales(w2_sc, w2_scales, nc.sync)
+        bases = [load_base(0)]
+        wg1_sb = sbuf("wg1_sb", [P, PACK, S], F32)
+        wg2_sb = sbuf("wg2_sb", [P, PACK, S], F32)
+        load_dealt(wg2_sb, wg2, 0, 1)
+        pages = [load_page(0)]
+        load_dealt(wg2_sb, wg2, 1, PACK)
+        w1_raw = []
+        for i in range(1, TILES):
+            bases.append(load_base(i))
+            pages.append(load_page(i))
+            if i <= HALVES:
+                w1_raw.append(load_raw("w1_raw%d" % (i - 1), w1[:, (i - 1) * HALF : i * HALF]))
+            if i == PACK:
+                load_dealt(wg1_sb, wg1, 0, PACK)
+
+        v2_codes, v2_plane = pick_table("v2", tab2_sb, tab2_sc, idx2)
+
+        def turns_of_half(b):
+            turns = sbuf("turns%d" % b, [P, PACK, PACK, P], F32, tag="turns")
+            for c in range(PACK):
+                z = bank("z%d_%d" % (b, c), 4 + c if b == 0 else 6 + c % 2)
+                js = slice(c * P, (c + 1) * P)
+                rs = slice(b * HALF, (b + 1) * HALF)
+                mx(z[:], v2_codes[:, js], v2_plane[:, js], w3_sb[:, rs], w3_sc[:, 0, rs], True, True)
+                nc.scalar.activation(
+                    out=turns[:, :, c, :], in_=z[:].rearrange("p (q t) -> p t q", t=PACK),
+                    func=ACT.Abs, scale=1.0 / (2.0 * math.pi), bias=minus_quarter[:],
+                )
+            return turns
+
+        def sine_tile(i, turns):
+            mine = turns[:, i % PACK, :, :].rearrange("p c q -> p (c q)")
+            whole = sbuf("whole%d" % i, [P, S], U32, tag="whole", bufs=2)
+            nc.scalar.activation(out=whole[:], in_=mine, func=ACT.Copy, scale=1.0, bias=0.25)
+            shift = sbuf("shift%d" % i, [P, S], F32, tag="shift", bufs=2)
+            nc.scalar.activation(out=shift[:], in_=whole[:], func=ACT.Copy, scale=-1.0, bias=0.25)
+            rest = bank("rest%d" % i, 4 + i % 2)
+            for c in range(PACK):
+                js = slice(c * P, (c + 1) * P)
+                nc.tensor.matmul(rest[:, js], lhsT=mine[:, js], rhs=ident[:], is_transpose=True, start=True, stop=False)
+                nc.tensor.matmul(rest[:, js], lhsT=shift[:, js], rhs=ident[:], is_transpose=True, start=False, stop=True)
+            sine = sbuf("sine%d" % i, [P, S], F32, tag="sine", bufs=2)
+            nc.scalar.activation(out=sine[:], in_=rest[:], func=ACT.Sin, scale=2.0 * math.pi)
+            h2 = sbuf("h2_%d" % i, [P, S], F32, tag="h2", bufs=4)
+            nc.vector.tensor_tensor(h2[:], sine[:], bases[i][:], ALU.add)
+            nc.vector.tensor_tensor(pages[i][:].indirect(idx4[:]), h2[:], wg2_sb[:, i % PACK, :], ALU.mult)
+
+        turns = turns_of_half(0)
+        v_codes, v_plane = pick_table("v", tab_sb, tab_sc, idx)
+
+        w2_codes = sbuf("w2_codes", [P, HALVES, 2 * H], U8)
+        w2_plane = sbuf("w2_plane", [P, HALVES, H], U8)
+        nc.vector.tensor_copy(
+            w2_codes[:].bitcast(U16).rearrange("p a (b t q) -> p (a b) q t", b=HALVES, t=PACK),
+            w2_sb[:].bitcast(U16).rearrange("p a (b q t) -> p (a b) q t", b=HALVES, t=PACK),
+        )
+        nc.vector.tensor_copy(
+            w2_plane[:].rearrange("p a (b t q) -> p (a b) q t", b=HALVES, t=PACK),
+            w2_sc[:].rearrange("p a (b q t) -> p (a b) q t", b=HALVES, t=PACK),
+        )
+
+        sine_tile(0, turns)
+        sine_tile(1, turns)
+
+        w1_codes, w1_plane = [], []
+        for b in range(HALVES):
+            grouped = woven("w1_woven%d" % b)
+            nc.scalar.copy(
+                out=grouped[:].rearrange("p (t m j) -> p m j t", t=PACK, j=PACK),
+                in_=w1_raw[b][:].rearrange("p j (m t) -> p m j t", t=PACK),
+            )
+            w1_codes.append(sbuf("w1_codes%d" % b, [P, HALF], U32))
+            w1_plane.append(sbuf("w1_plane%d" % b, [P, HALF], U8))
+            quantize(w1_codes[b][:], w1_plane[b][:], grouped[:])
+            sine_tile(2 + b, turns)
+
+        turns = turns_of_half(1)
+        sine_tile(PACK, turns)
+
+        t_codes, t_plane = [], []
+        for b in range(HALVES):
+            tanh_y = sbuf("tanh_y%d" % b, [P, S, PACK], F32, tag="raw", bufs=2)
+            for c in range(PACK):
+                y = bank("y%d_%d" % (b, c), c)
+                js = slice(c * P, (c + 1) * P)
+                for t in range(PACK):
+                    ts = slice(t * P, (t + 1) * P)
+                    mx(y[:, ts], w1_codes[b][:, ts], w1_plane[b][:, ts], v_codes[:, js], v_plane[:, js], True, True)
+                nc.scalar.activation(out=tanh_y[:, js, :], in_=y[:].rearrange("p (t j) -> p j t", t=PACK), func=ACT.Tanh)
+            grouped = woven("t_woven%d" % b)
+            nc.vector.tensor_tensor(
+                grouped[:].rearrange("p (j t) -> p j t", t=PACK),
+                tanh_y[:], gt_sb[:, b : b + 1, :].to_broadcast([P, S, PACK]), ALU.mult,
+            )
+            t_codes.append(sbuf("t_codes%d" % b, [P, S], U32))
+            t_plane.append(sbuf("t_plane%d" % b, [P, S], U8))
+            quantize(t_codes[b][:], t_plane[b][:], grouped[:])
+        wo_raw = [load_raw("wo_raw%d" % b, wo[b * HALF : (b + 1) * HALF, :]) for b in range(HALVES)]
+        sine_tile(PACK + 1, turns)
+
+        def thermistor_tile(i):
+            b, ts = i // PACK, slice((i % PACK) * P, (i % PACK + 1) * P)
+            acc = bank("h1_acc%d" % i, i % PACK)
+            mx(acc[:], w1_codes[b][:, ts], w1_plane[b][:, ts], v_codes[:], v_plane[:], True, False)
+            for a in range(HALVES):
+                mx(
+                    acc[:], w2_codes[:, a, 2 * P * i : 2 * P * (i + 1)], w2_plane[:, a, P * i : P * (i + 1)],
+                    t_codes[a][:], t_plane[a][:], False, a == HALVES - 1, lhs_dtype=FP4X4,
+                )
+            h1 = sbuf("h1_%d" % i, [P, S], F32, tag="h1", bufs=4)
+            nc.scalar.copy(out=h1[:], in_=acc[:])
+            return h1
+
+        x_rows = [sbuf("x_rows%d" % b, [P, PACK, PN], BF16, tag="wide", bufs=2) for b in range(HALVES)]
+        x_codes = [sbuf("x_codes%d" % b, [P, PN], U32, tag="codes", bufs=2) for b in range(HALVES)]
+        x_plane = [sbuf("x_plane%d" % b, [P, PN], U8) for b in range(HALVES)]
+
+        def place_and_pick(i):
+            h1 = thermistor_tile(i)
+            nc.vector.tensor_tensor(pages[i][:].indirect(idx3[:]), h1[:], wg1_sb[:, i % PACK, :], ALU.mult)
+            if i == TILES - 1:
+                parts = []
+                for q in range(4):
+                    parts.append(sbuf("picked_last%d" % q, [P, QUARTER], F32, tag="h2", bufs=4))
+                    cols = slice(q * QUARTER // 16, (q + 1) * QUARTER // 16)
+                    nc.vector.tensor_copy(parts[q][:], pages[i][:].indirect(idx5[:, cols]))
+                return parts
+            picked = sbuf("picked%d" % i, [P, PN], F32, tag="picked", bufs=3)
+            nc.vector.tensor_copy(picked[:], pages[i][:].indirect(idx5[:]))
+            return picked
+
+        def gain_slots(i, j0, j1, picked):
+            b, t = i // PACK, i % PACK
+            nc.scalar.activation(out=picked[:], in_=picked[:], func=ACT.Abs)
+            nc.scalar.activation(
+                out=x_rows[b][:, t, j0:j1], in_=picked[:], func=ACT.Copy, scale=gx_sb[:, b, t : t + 1]
+            )
+
+        def quantize_x(b, j0, j1, copy):
+            grouped = woven("x_woven%d_%d" % (b, j0))[:, 0 : PACK * (j1 - j0)]
+            copy(
+                grouped.rearrange("p (c i t) -> p c t i", i=4, t=PACK),
+                x_rows[b][:, :, j0:j1].rearrange("p t (c i) -> p c t i", i=4),
+            )
+            quantize(x_codes[b][:, j0:j1], x_plane[b][:, j0:j1], grouped)
+
+        wo_codes, wo_plane = [], []
+        picks = [place_and_pick(i) for i in range(AHEAD)]
+        for i in range(TILES - 1):
+            if i < 2:
+                sine_tile(PACK + 2 + i, turns)
+            if i + AHEAD < TILES:
+                picks.append(place_and_pick(i + AHEAD))
+            gain_slots(i, 0, PN, picks[i])
+            if i == PACK - 1:
+                for h in range(2):
+                    quantize_x(0, h * HALF, (h + 1) * HALF, nc.scalar.copy)
+            if i in (1, 2):
+                b = i - 1
+                grouped = woven("wo_woven%d" % b)
+                nc.scalar.copy(
+                    out=grouped[:].rearrange("p (c i j) -> p c j i", i=4, j=PACK),
+                    in_=wo_raw[b][:].rearrange("p j (c i) -> p c j i", i=4),
+                )
+                wo_codes.append(sbuf("wo_codes%d" % b, [P, N], U32))
+                wo_plane.append(sbuf("wo_plane%d" % b, [P, N], U8))
+                quantize(wo_codes[b][:], wo_plane[b][:], grouped[:])
+
+        def score_pass(acc, b, pair, q):
+            js = slice(q * QUARTER, (q + 1) * QUARTER)
+            for u in range(2):
+                ns = slice((2 * pair + u) * P, (2 * pair + u + 1) * P)
+                mx(
+                    acc[:, u * QUARTER : (u + 1) * QUARTER], wo_codes[b][:, ns], wo_plane[b][:, ns],
+                    x_codes[b][:, js], x_plane[b][:, js], b == 0 and u == 0, b == 1 and u == 1,
+                )
+
+        scores = {}
+        for q in range(4):
+            for pair in range(2):
+                scores[q, pair] = bank("score%d_%d" % (q, pair), (2 * q + pair + 4) % 8)
+                score_pass(scores[q, pair], 0, pair, q)
+
+        for q in range(4):
+            gain_slots(TILES - 1, q * QUARTER, (q + 1) * QUARTER, picks[TILES - 1][q])
+        for q in range(4):
+            j0, j1 = q * QUARTER, (q + 1) * QUARTER
+            quantize_x(1, j0, j1, nc.vector.tensor_copy)
+            for pair in range(2):
+                score_pass(scores[q, pair], 1, pair, q)
+                result = sbuf("result%d_%d" % (q, pair), [P, 2, QUARTER], F32, tag="h1", bufs=4)
+                nc.scalar.activation(
+                    out=result[:].rearrange("p u j -> p (u j)"), in_=scores[q, pair][:], func=ACT.Tanh
+                )
+                nc.sync.dma_start(
+                    out[2 * pair * P : 2 * (pair + 1) * P, j0:j1].rearrange("(u p) j -> p u j", u=2), result[:]
+                )

@@ -24,7 +24,11 @@ HALF = P * PACK
 HALVES = H // HALF
 TILES = H // P
 QUARTER = PN // 4
-AHEAD = 2
+AHEAD = 3
+RING = 2
+ADD_ON_VECTOR = 5
+EARLY = 6
+SINE_ORDER = [PACK * b + t for t in range(PACK) for b in range(HALVES)]
 
 
 def tile_list_embankment_slot_board_kernel(
@@ -58,16 +62,16 @@ def tile_list_embankment_slot_board_kernel(
             nc.vector.memset(dst[:].bitcast(I32), 0)
             return dst
 
-        def load_scales(dst, src, queue):
+        def load_scales(dst, src, queue, quadrants=range(4)):
             words = dst[:].bitcast(I32)
             rows = src.bitcast(I32).rearrange("a r n -> r a n")
-            for q in range(4):
+            for q in quadrants:
                 queue.dma_start(words[32 * q : 32 * q + 4, :, :], rows[4 * q : 4 * q + 4, :, :])
 
-        def load_dealt(dst, src, t0, t1):
+        def load_dealt(dst, src, t0, t1, queue):
             rows = src.rearrange("(p t) j -> p t j", t=PACK)
             for q in range(4):
-                nc.sync.dma_start(dst[32 * q : 32 * (q + 1), t0:t1, :], rows[:, t0:t1, :])
+                queue.dma_start(dst[32 * q : 32 * (q + 1), t0:t1, :], rows[:, t0:t1, :])
 
         def rows_of(src, i):
             return src.rearrange("(b p t) c -> b t p c", b=HALVES, t=PACK)[i // PACK, i % PACK, :, :]
@@ -104,89 +108,124 @@ def tile_list_embankment_slot_board_kernel(
                 rhs=rhs.bitcast(FP8X4), rhs_scale=rhs_scale, start=start, stop=stop,
             )
 
-        def pick_table(name, words, scales, idx):
+        def pick_table(name, words, scales, idx, pieces):
             codes = sbuf(name + "_codes", [P, S], U32)
             plane = sbuf(name + "_plane", [P, S], U8)
-            nc.vector.tensor_copy(codes[:], words[:].bitcast(U32).indirect(idx[:]))
-            nc.vector.tensor_copy(plane[:], scales[:, 0, :].indirect(idx[:]))
+            n = S // pieces
+            for j in range(0, S, n):
+                entries = idx[:, j // 16 : (j + n) // 16]
+                nc.vector.tensor_copy(codes[:, j : j + n], words[:].bitcast(U32).indirect(entries))
+                nc.vector.tensor_copy(plane[:, j : j + n], scales[:, 0, :].indirect(entries))
             return codes, plane
 
         tab2_sc = zeroed_plane("tab2_sc", tab2_scales)
         w3_sc = zeroed_plane("w3_sc", w3_scales)
-        tab_sc = zeroed_plane("tab_sc", tab_scales)
         w2_sc = zeroed_plane("w2_sc", w2_scales)
+        tab_sc = zeroed_plane("tab_sc", tab_scales)
         minus_quarter = sbuf("minus_quarter", [P, 1], F32)
         nc.vector.memset(minus_quarter[:], -0.25)
         warm = sbuf("warm", [P, 1], F32)
         nc.scalar.activation(out=warm[:], in_=minus_quarter[:], func=ACT.Silu)
 
+        wg1_sb = sbuf("wg1_sb", [P, PACK, S], F32)
+        wg2_sb = sbuf("wg2_sb", [P, PACK, S], F32)
+        ident = sbuf("ident", [P, P], F32)
+        make_identity(nc, ident[:])
+        load_scales(w3_sc, w3_scales, nc.gpsimd, (2, 3))
+        load_dealt(wg2_sb, wg2, 1, PACK, nc.gpsimd)
         idx2 = load_list("idx2", offs2)
-        gt_sb = load_gain("gt_sb", gt)
-        gx_sb = load_gain("gx_sb", gx)
-        idx = load_list("idx", offs)
         idx4 = load_list("idx4", offs4)
+        idx = load_list("idx", offs)
+        gt_sb = load_gain("gt_sb", gt)
         idx3 = load_list("idx3", offs3)
+        gx_sb = load_gain("gx_sb", gx)
         tab2_sb = load_words("tab2_sb", tab2_words, "wide")
         w3_sb = load_words("w3_sb", w3_words, "codes")
         load_scales(tab2_sc, tab2_scales, nc.sync)
-        load_scales(w3_sc, w3_scales, nc.gpsimd)
-        tab_sb = load_words("tab_sb", tab_words, "wide")
-        idx5 = load_list("idx5", offs5)
-        load_scales(tab_sc, tab_scales, nc.sync)
-        ident = sbuf("ident", [P, P], F32)
-        make_identity(nc, ident[:])
+        load_scales(w3_sc, w3_scales, nc.sync, (0, 1))
         w2_sb = sbuf("w2_sb", [P, HALVES, H // 2], I32, tag="codes", bufs=2)
         nc.sync.dma_start(w2_sb[:], w2_words.bitcast(I32).rearrange("a p n -> p a n"))
         load_scales(w2_sc, w2_scales, nc.sync)
-        bases = [load_base(0)]
-        wg1_sb = sbuf("wg1_sb", [P, PACK, S], F32)
-        wg2_sb = sbuf("wg2_sb", [P, PACK, S], F32)
-        load_dealt(wg2_sb, wg2, 0, 1)
-        pages = [load_page(0)]
-        load_dealt(wg2_sb, wg2, 1, PACK)
-        w1_raw = []
-        for i in range(1, TILES):
-            bases.append(load_base(i))
-            pages.append(load_page(i))
-            if i <= HALVES:
-                w1_raw.append(load_raw("w1_raw%d" % (i - 1), w1[:, (i - 1) * HALF : i * HALF]))
-            if i == PACK:
-                load_dealt(wg1_sb, wg1, 0, PACK)
+        bases, pages, w1_raw = {}, {}, []
 
-        v2_codes, v2_plane = pick_table("v2", tab2_sb, tab2_sc, idx2)
+        def load_tile(i):
+            bases[i] = load_base(i)
+            pages[i] = load_page(i)
 
-        def turns_of_half(b):
-            turns = sbuf("turns%d" % b, [P, PACK, PACK, P], F32, tag="turns")
-            for c in range(PACK):
-                z = bank("z%d_%d" % (b, c), 4 + c if b == 0 else 6 + c % 2)
-                js = slice(c * P, (c + 1) * P)
-                rs = slice(b * HALF, (b + 1) * HALF)
-                mx(z[:], v2_codes[:, js], v2_plane[:, js], w3_sb[:, rs], w3_sc[:, 0, rs], True, True)
-                nc.scalar.activation(
-                    out=turns[:, :, c, :], in_=z[:].rearrange("p (q t) -> p t q", t=PACK),
-                    func=ACT.Abs, scale=1.0 / (2.0 * math.pi), bias=minus_quarter[:],
-                )
-            return turns
+        def load_w1(b):
+            w1_raw.append(load_raw("w1_raw%d" % b, w1[:, b * HALF : (b + 1) * HALF]))
 
-        def sine_tile(i, turns):
-            mine = turns[:, i % PACK, :, :].rearrange("p c q -> p (c q)")
+        load_tile(SINE_ORDER[0])
+        load_dealt(wg2_sb, wg2, 0, 1, nc.sync)
+        tab_sb = load_words("tab_sb", tab_words, "wide")
+        load_scales(tab_sc, tab_scales, nc.sync)
+        load_tile(SINE_ORDER[1])
+        load_w1(0)
+        load_tile(SINE_ORDER[2])
+        load_w1(1)
+        load_tile(SINE_ORDER[3])
+        load_tile(SINE_ORDER[4])
+        idx5 = load_list("idx5", offs5)
+        load_dealt(wg1_sb, wg1, 0, PACK, nc.sync)
+        for i in SINE_ORDER[5:]:
+            load_tile(i)
+
+        gx_sign = sbuf("gx_sign", [P, HALVES, PACK], F32)
+        nc.vector.tensor_scalar(gx_sign[:], gx_sb[:], 0.0, 2.0, ALU.is_ge, ALU.mult)
+        nc.vector.tensor_scalar(gx_sign[:], gx_sign[:], -1.0, None, ALU.add)
+
+        v2_codes, v2_plane = pick_table("v2", tab2_sb, tab2_sc, idx2, 2)
+
+        turns = [sbuf("turns%d" % b, [P, PACK, PACK, P], F32) for b in range(HALVES)]
+
+        def turns_of_chunk(b, c):
+            z = bank("z%d_%d" % (b, c), (4 + PACK * b + c) % 8)
+            js = slice(c * P, (c + 1) * P)
+            rs = slice(b * HALF, (b + 1) * HALF)
+            mx(z[:], v2_codes[:, js], v2_plane[:, js], w3_sb[:, rs], w3_sc[:, 0, rs], True, True)
+            nc.scalar.activation(
+                out=turns[b][:, :, c, :], in_=z[:].rearrange("p (q t) -> p t q", t=PACK),
+                func=ACT.Abs, scale=1.0 / (2.0 * math.pi), bias=minus_quarter[:],
+            )
+
+        def add_turned(dst, left, right, j0, j1):
+            for j in range(j0, j1, P):
+                js = slice(j, j + P)
+                nc.tensor.matmul(dst[:, js], lhsT=left[:, js], rhs=ident[:], is_transpose=True, start=True, stop=False)
+                nc.tensor.matmul(dst[:, js], lhsT=right[:, js], rhs=ident[:], is_transpose=True, start=False, stop=True)
+
+        def sine_tile(step, pieces=1):
+            i = SINE_ORDER[step]
+            mine = turns[i // PACK][:, i % PACK, :, :].rearrange("p c q -> p (c q)")
             whole = sbuf("whole%d" % i, [P, S], U32, tag="whole", bufs=2)
-            nc.scalar.activation(out=whole[:], in_=mine, func=ACT.Copy, scale=1.0, bias=0.25)
             shift = sbuf("shift%d" % i, [P, S], F32, tag="shift", bufs=2)
-            nc.scalar.activation(out=shift[:], in_=whole[:], func=ACT.Copy, scale=-1.0, bias=0.25)
-            rest = bank("rest%d" % i, 4 + i % 2)
-            for c in range(PACK):
-                js = slice(c * P, (c + 1) * P)
-                nc.tensor.matmul(rest[:, js], lhsT=mine[:, js], rhs=ident[:], is_transpose=True, start=True, stop=False)
-                nc.tensor.matmul(rest[:, js], lhsT=shift[:, js], rhs=ident[:], is_transpose=True, start=False, stop=True)
             sine = sbuf("sine%d" % i, [P, S], F32, tag="sine", bufs=2)
-            nc.scalar.activation(out=sine[:], in_=rest[:], func=ACT.Sin, scale=2.0 * math.pi)
             h2 = sbuf("h2_%d" % i, [P, S], F32, tag="h2", bufs=4)
-            nc.vector.tensor_tensor(h2[:], sine[:], bases[i][:], ALU.add)
-            nc.vector.tensor_tensor(pages[i][:].indirect(idx4[:]), h2[:], wg2_sb[:, i % PACK, :], ALU.mult)
-
-        turns = turns_of_half(0)
-        v_codes, v_plane = pick_table("v", tab_sb, tab_sc, idx)
+            n = S // pieces
+            for j in range(0, S, n):
+                js = slice(j, j + n)
+                if step == 0:
+                    for c in range(j // P, (j + n) // P):
+                        turns_of_chunk(0, c)
+                nc.scalar.activation(out=whole[:, js], in_=mine[:, js], func=ACT.Copy, scale=1.0, bias=0.25)
+                nc.scalar.activation(out=shift[:, js], in_=whole[:, js], func=ACT.Copy, scale=-1.0, bias=0.25)
+                rest = bank("rest%d_%d" % (i, j), 4 + (step + j // n) % 2)
+                add_turned(rest, mine, shift, j, j + n)
+                nc.scalar.activation(out=sine[:, js], in_=rest[:, js], func=ACT.Sin, scale=2.0 * math.pi)
+                if step < ADD_ON_VECTOR:
+                    nc.vector.tensor_tensor(h2[:, js], sine[:, js], bases[i][:, js], ALU.add)
+                else:
+                    turned = bank("turned%d" % i, 6)
+                    add_turned(turned, sine, bases[i], 0, S)
+                    h2_turned = sbuf("h2_turned%d" % i, [P, S], F32, tag="h2_turned", bufs=2)
+                    nc.scalar.copy(out=h2_turned[:], in_=turned[:])
+                    back = bank("back%d" % i, 7)
+                    for c in range(PACK):
+                        cs = slice(c * P, (c + 1) * P)
+                        nc.tensor.transpose(back[:, cs], h2_turned[:, cs], ident[:])
+                    nc.scalar.copy(out=h2[:], in_=back[:])
+                entries = idx4[:, j // 16 : (j + n) // 16]
+                nc.vector.tensor_tensor(pages[i][:].indirect(entries), h2[:, js], wg2_sb[:, i % PACK, js], ALU.mult)
 
         w2_codes = sbuf("w2_codes", [P, HALVES, 2 * H], U8)
         w2_plane = sbuf("w2_plane", [P, HALVES, H], U8)
@@ -199,10 +238,14 @@ def tile_list_embankment_slot_board_kernel(
             w2_sc[:].rearrange("p a (b q t) -> p (a b) q t", b=HALVES, t=PACK),
         )
 
-        sine_tile(0, turns)
-        sine_tile(1, turns)
+        sine_tile(0, 2)
+        for c in range(PACK):
+            turns_of_chunk(1, c)
+        v_codes, v_plane = pick_table("v", tab_sb, tab_sc, idx, 1)
+        sine_tile(1)
+        sine_tile(2)
 
-        w1_codes, w1_plane = [], []
+        w1_codes, w1_plane, t_codes, t_plane = [], [], [], []
         for b in range(HALVES):
             grouped = woven("w1_woven%d" % b)
             nc.scalar.copy(
@@ -212,13 +255,7 @@ def tile_list_embankment_slot_board_kernel(
             w1_codes.append(sbuf("w1_codes%d" % b, [P, HALF], U32))
             w1_plane.append(sbuf("w1_plane%d" % b, [P, HALF], U8))
             quantize(w1_codes[b][:], w1_plane[b][:], grouped[:])
-            sine_tile(2 + b, turns)
-
-        turns = turns_of_half(1)
-        sine_tile(PACK, turns)
-
-        t_codes, t_plane = [], []
-        for b in range(HALVES):
+            sine_tile(3 + b)
             tanh_y = sbuf("tanh_y%d" % b, [P, S, PACK], F32, tag="raw", bufs=2)
             for c in range(PACK):
                 y = bank("y%d_%d" % (b, c), c)
@@ -236,17 +273,18 @@ def tile_list_embankment_slot_board_kernel(
             t_plane.append(sbuf("t_plane%d" % b, [P, S], U8))
             quantize(t_codes[b][:], t_plane[b][:], grouped[:])
         wo_raw = [load_raw("wo_raw%d" % b, wo[b * HALF : (b + 1) * HALF, :]) for b in range(HALVES)]
-        sine_tile(PACK + 1, turns)
+        for step in range(5, EARLY):
+            sine_tile(step)
 
         def thermistor_tile(i):
             b, ts = i // PACK, slice((i % PACK) * P, (i % PACK + 1) * P)
             acc = bank("h1_acc%d" % i, i % PACK)
-            mx(acc[:], w1_codes[b][:, ts], w1_plane[b][:, ts], v_codes[:], v_plane[:], True, False)
-            for a in range(HALVES):
+            for a in reversed(range(HALVES)):
                 mx(
                     acc[:], w2_codes[:, a, 2 * P * i : 2 * P * (i + 1)], w2_plane[:, a, P * i : P * (i + 1)],
-                    t_codes[a][:], t_plane[a][:], False, a == HALVES - 1, lhs_dtype=FP4X4,
+                    t_codes[a][:], t_plane[a][:], a == HALVES - 1, False, lhs_dtype=FP4X4,
                 )
+            mx(acc[:], w1_codes[b][:, ts], w1_plane[b][:, ts], v_codes[:], v_plane[:], False, True)
             h1 = sbuf("h1_%d" % i, [P, S], F32, tag="h1", bufs=4)
             nc.scalar.copy(out=h1[:], in_=acc[:])
             return h1
@@ -255,25 +293,23 @@ def tile_list_embankment_slot_board_kernel(
         x_codes = [sbuf("x_codes%d" % b, [P, PN], U32, tag="codes", bufs=2) for b in range(HALVES)]
         x_plane = [sbuf("x_plane%d" % b, [P, PN], U8) for b in range(HALVES)]
 
-        def place_and_pick(i):
+        def place(i):
             h1 = thermistor_tile(i)
             nc.vector.tensor_tensor(pages[i][:].indirect(idx3[:]), h1[:], wg1_sb[:, i % PACK, :], ALU.mult)
-            if i == TILES - 1:
-                parts = []
-                for q in range(4):
-                    parts.append(sbuf("picked_last%d" % q, [P, QUARTER], F32, tag="h2", bufs=4))
-                    cols = slice(q * QUARTER // 16, (q + 1) * QUARTER // 16)
-                    nc.vector.tensor_copy(parts[q][:], pages[i][:].indirect(idx5[:, cols]))
-                return parts
-            picked = sbuf("picked%d" % i, [P, PN], F32, tag="picked", bufs=3)
-            nc.vector.tensor_copy(picked[:], pages[i][:].indirect(idx5[:]))
+
+        def pick(i, j0, j1, tag, bufs=2):
+            picked = sbuf("picked%d_%d" % (i, j0), [P, j1 - j0], F32, tag=tag, bufs=bufs)
+            nc.vector.tensor_copy(picked[:], pages[i][:].indirect(idx5[:, j0 // 16 : j1 // 16]))
             return picked
 
         def gain_slots(i, j0, j1, picked):
             b, t = i // PACK, i % PACK
-            nc.scalar.activation(out=picked[:], in_=picked[:], func=ACT.Abs)
-            nc.scalar.activation(
-                out=x_rows[b][:, t, j0:j1], in_=picked[:], func=ACT.Copy, scale=gx_sb[:, b, t : t + 1]
+            nc.scalar.activation(out=x_rows[b][:, t, j0:j1], in_=picked[:], func=ACT.Abs, scale=gx_sb[:, b, t : t + 1])
+
+        def weave_pair(u, j0, j1, copy):
+            copy(
+                last_woven[:, j0:j1, 2 * u : 2 * u + 2].rearrange("p (c i) t -> p c t i", i=4),
+                x_rows[1][:, 2 * u : 2 * u + 2, j0:j1].rearrange("p t (c i) -> p c t i", i=4),
             )
 
         def quantize_x(b, j0, j1, copy):
@@ -284,23 +320,39 @@ def tile_list_embankment_slot_board_kernel(
             )
             quantize(x_codes[b][:, j0:j1], x_plane[b][:, j0:j1], grouped)
 
+        last_woven = sbuf("last_woven", [P, PN, PACK], BF16, tag="raw", bufs=2)
+
         wo_codes, wo_plane = [], []
-        picks = [place_and_pick(i) for i in range(AHEAD)]
+        for i in range(AHEAD):
+            place(i)
+        picks = [pick(i, 0, PN, "picked") for i in range(2)]
         for i in range(TILES - 1):
-            if i < 2:
-                sine_tile(PACK + 2 + i, turns)
-            if i + AHEAD < TILES:
-                picks.append(place_and_pick(i + AHEAD))
+            if EARLY + i < TILES:
+                sine_tile(EARLY + i)
+            if i + AHEAD < TILES - 1:
+                place(i + AHEAD)
             gain_slots(i, 0, PN, picks[i])
+            if i + 2 < TILES - 1:
+                picks.append(pick(i + 2, 0, PN, "picked"))
+            if i + 2 == TILES - 2:
+                place(TILES - 1)
             if i == PACK - 1:
                 for h in range(2):
                     quantize_x(0, h * HALF, (h + 1) * HALF, nc.scalar.copy)
+            if i == PACK + 1:
+                weave_pair(0, 0, PN, nc.scalar.copy)
             if i in (1, 2):
                 b = i - 1
+                wo_rows = woven("wo_rows%d" % b)
+                for t in range(PACK):
+                    nc.scalar.activation(
+                        out=wo_rows[:, t * N : (t + 1) * N], in_=wo_raw[b][:, t, :], func=ACT.Copy,
+                        scale=gx_sign[:, b, t : t + 1],
+                    )
                 grouped = woven("wo_woven%d" % b)
                 nc.scalar.copy(
                     out=grouped[:].rearrange("p (c i j) -> p c j i", i=4, j=PACK),
-                    in_=wo_raw[b][:].rearrange("p j (c i) -> p c j i", i=4),
+                    in_=wo_rows[:].rearrange("p (j c i) -> p c j i", i=4, j=PACK),
                 )
                 wo_codes.append(sbuf("wo_codes%d" % b, [P, N], U32))
                 wo_plane.append(sbuf("wo_plane%d" % b, [P, N], U8))
@@ -321,14 +373,19 @@ def tile_list_embankment_slot_board_kernel(
                 scores[q, pair] = bank("score%d_%d" % (q, pair), (2 * q + pair + 4) % 8)
                 score_pass(scores[q, pair], 0, pair, q)
 
-        for q in range(4):
-            gain_slots(TILES - 1, q * QUARTER, (q + 1) * QUARTER, picks[TILES - 1][q])
+        parts = [pick(TILES - 1, q * QUARTER, (q + 1) * QUARTER, "part", RING) for q in range(RING)]
         for q in range(4):
             j0, j1 = q * QUARTER, (q + 1) * QUARTER
-            quantize_x(1, j0, j1, nc.vector.tensor_copy)
+            gain_slots(TILES - 1, j0, j1, parts[q])
+            weave_pair(1, j0, j1, nc.vector.tensor_copy)
+            quantize(x_codes[1][:, j0:j1], x_plane[1][:, j0:j1], last_woven[:, j0:j1, :].rearrange("p j t -> p (j t)"))
+            if q + RING < 4:
+                parts.append(pick(TILES - 1, j0 + RING * QUARTER, j1 + RING * QUARTER, "part", RING))
+        for q in range(4):
+            j0, j1 = q * QUARTER, (q + 1) * QUARTER
             for pair in range(2):
                 score_pass(scores[q, pair], 1, pair, q)
-                result = sbuf("result%d_%d" % (q, pair), [P, 2, QUARTER], F32, tag="h1", bufs=4)
+                result = sbuf("result%d_%d" % (q, pair), [P, 2, QUARTER], F32, tag="page%d" % (2 * q + pair))
                 nc.scalar.activation(
                     out=result[:].rearrange("p u j -> p (u j)"), in_=scores[q, pair][:], func=ACT.Tanh
                 )

@@ -24,11 +24,17 @@ HALF = P * PACK
 HALVES = H // HALF
 TILES = H // P
 QUARTER = PN // 4
-AHEAD = 3
+AHEAD = 2
 RING = 2
+PICKS = 4
+LAG = 0
+WO_STEP = 1
+LAST_TAG = "h1"
 ADD_ON_VECTOR = 5
 EARLY = 6
-SINE_ORDER = [PACK * b + t for t in range(PACK) for b in range(HALVES)]
+SINE_ORDER = list(range(TILES))
+LOADS = "tab p1 a0 p2 p3 a1 p4 p5 wg o0 p6 o1 p7"
+WO0 = 0
 
 
 def tile_list_embankment_slot_board_kernel(
@@ -52,8 +58,8 @@ def tile_list_embankment_slot_board_kernel(
             nc.sync.dma_start(dst[:], src)
             return dst
 
-        def load_words(name, src, tag):
-            dst = sbuf(name, [P, src.shape[2]], I32, tag=tag, bufs=2)
+        def load_words(name, src, tag, bufs):
+            dst = sbuf(name, [P, src.shape[2]], I32, tag=tag, bufs=bufs)
             nc.sync.dma_start(dst[:], src[0].rearrange("p n i -> p (n i)").bitcast(I32))
             return dst
 
@@ -62,11 +68,11 @@ def tile_list_embankment_slot_board_kernel(
             nc.vector.memset(dst[:].bitcast(I32), 0)
             return dst
 
-        def load_scales(dst, src, queue, quadrants=range(4)):
+        def load_scales(dst, src):
             words = dst[:].bitcast(I32)
             rows = src.bitcast(I32).rearrange("a r n -> r a n")
-            for q in quadrants:
-                queue.dma_start(words[32 * q : 32 * q + 4, :, :], rows[4 * q : 4 * q + 4, :, :])
+            for q in range(4):
+                nc.sync.dma_start(words[32 * q : 32 * q + 4, :, :], rows[4 * q : 4 * q + 4, :, :])
 
         def load_dealt(dst, src, t0, t1, queue):
             rows = src.rearrange("(p t) j -> p t j", t=PACK)
@@ -86,8 +92,8 @@ def tile_list_embankment_slot_board_kernel(
             nc.sync.dma_start(dst[:], rows_of(base, i))
             return dst
 
-        def load_raw(name, src):
-            dst = sbuf(name, [P, PACK, HALF], F32, tag="raw", bufs=2)
+        def load_raw(name, src, tag, bufs):
+            dst = sbuf(name, [P, PACK, HALF], F32, tag=tag, bufs=bufs)
             nc.sync.dma_start(dst[:], src.rearrange("(p j) c -> p j c", j=PACK))
             return dst
 
@@ -127,59 +133,58 @@ def tile_list_embankment_slot_board_kernel(
         warm = sbuf("warm", [P, 1], F32)
         nc.scalar.activation(out=warm[:], in_=minus_quarter[:], func=ACT.Silu)
 
-        wg1_sb = sbuf("wg1_sb", [P, PACK, S], F32)
         wg2_sb = sbuf("wg2_sb", [P, PACK, S], F32)
         ident = sbuf("ident", [P, P], F32)
         make_identity(nc, ident[:])
-        load_scales(w3_sc, w3_scales, nc.gpsimd, (2, 3))
         load_dealt(wg2_sb, wg2, 1, PACK, nc.gpsimd)
         idx2 = load_list("idx2", offs2)
-        idx4 = load_list("idx4", offs4)
-        idx = load_list("idx", offs)
-        gt_sb = load_gain("gt_sb", gt)
-        idx3 = load_list("idx3", offs3)
-        gx_sb = load_gain("gx_sb", gx)
-        tab2_sb = load_words("tab2_sb", tab2_words, "wide")
-        w3_sb = load_words("w3_sb", w3_words, "codes")
-        load_scales(tab2_sc, tab2_scales, nc.sync)
-        load_scales(w3_sc, w3_scales, nc.sync, (0, 1))
+        tab2_sb = load_words("tab2_sb", tab2_words, "wide0", 1)
+        load_scales(tab2_sc, tab2_scales)
+        w3_sb = load_words("w3_sb", w3_words, "codes", 2)
+        load_scales(w3_sc, w3_scales)
         w2_sb = sbuf("w2_sb", [P, HALVES, H // 2], I32, tag="codes", bufs=2)
         nc.sync.dma_start(w2_sb[:], w2_words.bitcast(I32).rearrange("a p n -> p a n"))
-        load_scales(w2_sc, w2_scales, nc.sync)
-        bases, pages, w1_raw = {}, {}, []
+        load_scales(w2_sc, w2_scales)
+        bases, pages, w1_raw, wo_raw = {}, {}, [], []
 
         def load_tile(i):
-            bases[i] = load_base(i)
             pages[i] = load_page(i)
+            bases[i] = load_base(i)
 
         def load_w1(b):
-            w1_raw.append(load_raw("w1_raw%d" % b, w1[:, b * HALF : (b + 1) * HALF]))
+            w1_raw.append(load_raw("w1_raw%d" % b, w1[:, b * HALF : (b + 1) * HALF], "stage%d" % (b + 1), 1))
 
-        load_tile(SINE_ORDER[0])
+        def load_wo(b):
+            wo_raw.append(load_raw("wo_raw%d" % b, wo[b * HALF : (b + 1) * HALF, :], "wide%d" % b, 1))
+
+        idx4 = load_list("idx4", offs4)
+        bases[0] = load_base(0)
         load_dealt(wg2_sb, wg2, 0, 1, nc.sync)
-        tab_sb = load_words("tab_sb", tab_words, "wide")
-        load_scales(tab_sc, tab_scales, nc.sync)
-        load_tile(SINE_ORDER[1])
-        load_w1(0)
-        load_tile(SINE_ORDER[2])
-        load_w1(1)
-        load_tile(SINE_ORDER[3])
-        load_tile(SINE_ORDER[4])
-        idx5 = load_list("idx5", offs5)
-        load_dealt(wg1_sb, wg1, 0, PACK, nc.sync)
-        for i in SINE_ORDER[5:]:
-            load_tile(i)
-
-        gx_sign = sbuf("gx_sign", [P, HALVES, PACK], F32)
-        nc.vector.tensor_scalar(gx_sign[:], gx_sb[:], 0.0, 2.0, ALU.is_ge, ALU.mult)
-        nc.vector.tensor_scalar(gx_sign[:], gx_sign[:], -1.0, None, ALU.add)
+        pages[0] = load_page(0)
+        for item in LOADS.split():
+            if item == "tab":
+                tab_sb = load_words("tab_sb", tab_words, "tab", 1)
+                idx = load_list("idx", offs)
+                load_scales(tab_sc, tab_scales)
+            if item[0] == "p":
+                load_tile(int(item[1]))
+            if item[0] == "a":
+                load_w1(int(item[1]))
+            if item == "a0":
+                gt_sb = load_gain("gt_sb", gt)
+                gx_sb = load_gain("gx_sb", gx)
+            if item[0] == "o":
+                load_wo(int(item[1]))
+            if item == "wg":
+                idx3 = load_list("idx3", offs3)
+                idx5 = load_list("idx5", offs5)
 
         v2_codes, v2_plane = pick_table("v2", tab2_sb, tab2_sc, idx2, 2)
 
-        turns = [sbuf("turns%d" % b, [P, PACK, PACK, P], F32) for b in range(HALVES)]
+        turns = [sbuf("turns%d" % b, [P, PACK, PACK, P], F32, tag="stage%d" % b) for b in range(HALVES)]
 
         def turns_of_chunk(b, c):
-            z = bank("z%d_%d" % (b, c), (4 + PACK * b + c) % 8)
+            z = bank("z%d_%d" % (b, c), 4 + c if b == 0 else 6 + c % 2)
             js = slice(c * P, (c + 1) * P)
             rs = slice(b * HALF, (b + 1) * HALF)
             mx(z[:], v2_codes[:, js], v2_plane[:, js], w3_sb[:, rs], w3_sc[:, 0, rs], True, True)
@@ -200,10 +205,13 @@ def tile_list_embankment_slot_board_kernel(
             whole = sbuf("whole%d" % i, [P, S], U32, tag="whole", bufs=2)
             shift = sbuf("shift%d" % i, [P, S], F32, tag="shift", bufs=2)
             sine = sbuf("sine%d" % i, [P, S], F32, tag="sine", bufs=2)
-            h2 = sbuf("h2_%d" % i, [P, S], F32, tag="h2", bufs=4)
             n = S // pieces
             for j in range(0, S, n):
                 js = slice(j, j + n)
+                if pieces > 1:
+                    h2 = sbuf("h2_%d_%d" % (i, j), [P, n], F32, tag="h2_piece")
+                else:
+                    h2 = sbuf("h2_%d" % i, [P, S], F32, tag="h2", bufs=4)
                 if step == 0:
                     for c in range(j // P, (j + n) // P):
                         turns_of_chunk(0, c)
@@ -213,7 +221,7 @@ def tile_list_embankment_slot_board_kernel(
                 add_turned(rest, mine, shift, j, j + n)
                 nc.scalar.activation(out=sine[:, js], in_=rest[:, js], func=ACT.Sin, scale=2.0 * math.pi)
                 if step < ADD_ON_VECTOR:
-                    nc.vector.tensor_tensor(h2[:, js], sine[:, js], bases[i][:, js], ALU.add)
+                    nc.vector.tensor_tensor(h2[:], sine[:, js], bases[i][:, js], ALU.add)
                 else:
                     turned = bank("turned%d" % i, 6)
                     add_turned(turned, sine, bases[i], 0, S)
@@ -225,7 +233,7 @@ def tile_list_embankment_slot_board_kernel(
                         nc.tensor.transpose(back[:, cs], h2_turned[:, cs], ident[:])
                     nc.scalar.copy(out=h2[:], in_=back[:])
                 entries = idx4[:, j // 16 : (j + n) // 16]
-                nc.vector.tensor_tensor(pages[i][:].indirect(entries), h2[:, js], wg2_sb[:, i % PACK, js], ALU.mult)
+                nc.vector.tensor_tensor(pages[i][:].indirect(entries), h2[:], wg2_sb[:, i % PACK, js], ALU.mult)
 
         w2_codes = sbuf("w2_codes", [P, HALVES, 2 * H], U8)
         w2_plane = sbuf("w2_plane", [P, HALVES, H], U8)
@@ -239,9 +247,13 @@ def tile_list_embankment_slot_board_kernel(
         )
 
         sine_tile(0, 2)
-        for c in range(PACK):
-            turns_of_chunk(1, c)
         v_codes, v_plane = pick_table("v", tab_sb, tab_sc, idx, 1)
+        wg1_sb = sbuf("wg1_sb", [P, PACK, S], F32, tag="tab")
+        load_dealt(wg1_sb, wg1, 0, PACK, nc.gpsimd)
+        gx_sign = sbuf("gx_sign", [P, HALVES, PACK], F32)
+        nc.gpsimd.tensor_scalar(gx_sign[:], gx_sb[:], 0.0, 2.0, ALU.is_ge, ALU.mult)
+        nc.gpsimd.tensor_scalar(gx_sign[:], gx_sign[:], 1.0, -1.0, ALU.mult, ALU.add)
+
         sine_tile(1)
         sine_tile(2)
 
@@ -255,8 +267,11 @@ def tile_list_embankment_slot_board_kernel(
             w1_codes.append(sbuf("w1_codes%d" % b, [P, HALF], U32))
             w1_plane.append(sbuf("w1_plane%d" % b, [P, HALF], U8))
             quantize(w1_codes[b][:], w1_plane[b][:], grouped[:])
+            if b == 1:
+                for c in range(PACK):
+                    turns_of_chunk(1, c)
             sine_tile(3 + b)
-            tanh_y = sbuf("tanh_y%d" % b, [P, S, PACK], F32, tag="raw", bufs=2)
+            tanh_y = sbuf("tanh_y%d" % b, [P, S, PACK], F32, tag="stage%d" % (2 * b))
             for c in range(PACK):
                 y = bank("y%d_%d" % (b, c), c)
                 js = slice(c * P, (c + 1) * P)
@@ -272,7 +287,6 @@ def tile_list_embankment_slot_board_kernel(
             t_codes.append(sbuf("t_codes%d" % b, [P, S], U32))
             t_plane.append(sbuf("t_plane%d" % b, [P, S], U8))
             quantize(t_codes[b][:], t_plane[b][:], grouped[:])
-        wo_raw = [load_raw("wo_raw%d" % b, wo[b * HALF : (b + 1) * HALF, :]) for b in range(HALVES)]
         for step in range(5, EARLY):
             sine_tile(step)
 
@@ -285,11 +299,11 @@ def tile_list_embankment_slot_board_kernel(
                     t_codes[a][:], t_plane[a][:], a == HALVES - 1, False, lhs_dtype=FP4X4,
                 )
             mx(acc[:], w1_codes[b][:, ts], w1_plane[b][:, ts], v_codes[:], v_plane[:], False, True)
-            h1 = sbuf("h1_%d" % i, [P, S], F32, tag="h1", bufs=4)
+            h1 = sbuf("h1_%d" % i, [P, S], F32, tag="h1", bufs=4) if i < TILES - 1 or LAST_TAG == "h1" else sbuf("h1_%d" % i, [P, S], F32, tag="woven", bufs=3)
             nc.scalar.copy(out=h1[:], in_=acc[:])
             return h1
 
-        x_rows = [sbuf("x_rows%d" % b, [P, PACK, PN], BF16, tag="wide", bufs=2) for b in range(HALVES)]
+        x_rows = [sbuf("x_rows%d" % b, [P, PACK, PN], BF16, tag="wide%d" % b) for b in range(HALVES)]
         x_codes = [sbuf("x_codes%d" % b, [P, PN], U32, tag="codes", bufs=2) for b in range(HALVES)]
         x_plane = [sbuf("x_plane%d" % b, [P, PN], U8) for b in range(HALVES)]
 
@@ -320,43 +334,48 @@ def tile_list_embankment_slot_board_kernel(
             )
             quantize(x_codes[b][:, j0:j1], x_plane[b][:, j0:j1], grouped)
 
-        last_woven = sbuf("last_woven", [P, PN, PACK], BF16, tag="raw", bufs=2)
+        last_woven = sbuf("last_woven", [P, PN, PACK], BF16, tag="stage2")
 
         wo_codes, wo_plane = [], []
+
+        def quantize_wo(b):
+            wo_rows = woven("wo_rows%d" % b)
+            for t in range(PACK):
+                nc.scalar.activation(
+                    out=wo_rows[:, t * N : (t + 1) * N], in_=wo_raw[b][:, t, :], func=ACT.Copy,
+                    scale=gx_sign[:, b, t : t + 1],
+                )
+            grouped = woven("wo_woven%d" % b)
+            nc.scalar.copy(
+                out=grouped[:].rearrange("p (c i j) -> p c j i", i=4, j=PACK),
+                in_=wo_rows[:].rearrange("p (j c i) -> p c j i", i=4, j=PACK),
+            )
+            wo_codes.append(sbuf("wo_codes%d" % b, [P, N], U32))
+            wo_plane.append(sbuf("wo_plane%d" % b, [P, N], U8))
+            quantize(wo_codes[b][:], wo_plane[b][:], grouped[:])
+
+        quantize_wo(0)
         for i in range(AHEAD):
             place(i)
-        picks = [pick(i, 0, PN, "picked") for i in range(2)]
+        picks = [pick(i, 0, PN, "picked", PICKS) for i in range(AHEAD - LAG)]
         for i in range(TILES - 1):
             if EARLY + i < TILES:
                 sine_tile(EARLY + i)
-            if i + AHEAD < TILES - 1:
+            if i + AHEAD < TILES:
                 place(i + AHEAD)
-            gain_slots(i, 0, PN, picks[i])
-            if i + 2 < TILES - 1:
-                picks.append(pick(i + 2, 0, PN, "picked"))
-            if i + 2 == TILES - 2:
-                place(TILES - 1)
+            if LAG:
+                gain_slots(i, 0, PN, picks[i])
+            if i + AHEAD - LAG < TILES - 1:
+                picks.append(pick(i + AHEAD - LAG, 0, PN, "picked", PICKS))
+            if not LAG:
+                gain_slots(i, 0, PN, picks[i])
             if i == PACK - 1:
                 for h in range(2):
                     quantize_x(0, h * HALF, (h + 1) * HALF, nc.scalar.copy)
             if i == PACK + 1:
                 weave_pair(0, 0, PN, nc.scalar.copy)
-            if i in (1, 2):
-                b = i - 1
-                wo_rows = woven("wo_rows%d" % b)
-                for t in range(PACK):
-                    nc.scalar.activation(
-                        out=wo_rows[:, t * N : (t + 1) * N], in_=wo_raw[b][:, t, :], func=ACT.Copy,
-                        scale=gx_sign[:, b, t : t + 1],
-                    )
-                grouped = woven("wo_woven%d" % b)
-                nc.scalar.copy(
-                    out=grouped[:].rearrange("p (c i j) -> p c j i", i=4, j=PACK),
-                    in_=wo_rows[:].rearrange("p (j c i) -> p c j i", i=4, j=PACK),
-                )
-                wo_codes.append(sbuf("wo_codes%d" % b, [P, N], U32))
-                wo_plane.append(sbuf("wo_plane%d" % b, [P, N], U8))
-                quantize(wo_codes[b][:], wo_plane[b][:], grouped[:])
+            if i == WO_STEP:
+                quantize_wo(1)
 
         def score_pass(acc, b, pair, q):
             js = slice(q * QUARTER, (q + 1) * QUARTER)
@@ -373,14 +392,14 @@ def tile_list_embankment_slot_board_kernel(
                 scores[q, pair] = bank("score%d_%d" % (q, pair), (2 * q + pair + 4) % 8)
                 score_pass(scores[q, pair], 0, pair, q)
 
-        parts = [pick(TILES - 1, q * QUARTER, (q + 1) * QUARTER, "part", RING) for q in range(RING)]
+        parts = [pick(TILES - 1, q * QUARTER, (q + 1) * QUARTER, "sine", RING) for q in range(RING)]
         for q in range(4):
             j0, j1 = q * QUARTER, (q + 1) * QUARTER
             gain_slots(TILES - 1, j0, j1, parts[q])
             weave_pair(1, j0, j1, nc.vector.tensor_copy)
             quantize(x_codes[1][:, j0:j1], x_plane[1][:, j0:j1], last_woven[:, j0:j1, :].rearrange("p j t -> p (j t)"))
             if q + RING < 4:
-                parts.append(pick(TILES - 1, j0 + RING * QUARTER, j1 + RING * QUARTER, "part", RING))
+                parts.append(pick(TILES - 1, j0 + RING * QUARTER, j1 + RING * QUARTER, "sine", RING))
         for q in range(4):
             j0, j1 = q * QUARTER, (q + 1) * QUARTER
             for pair in range(2):

@@ -4,7 +4,7 @@ from contextlib import ExitStack
 import concourse.mybir as mybir
 from concourse.masks import make_identity
 
-K, T, S, H, T2, PN, N = 512, 2048, 512, 1024, 2048, 1024, 512
+K, S, H, T2, PN, N = 512, 512, 1024, 2048, 1024, 512
 FLOPS = 2 * (3 * K * H * S + H * H * S + H * N * PN)
 
 F32 = mybir.dt.float32
@@ -23,18 +23,15 @@ PACK = 4
 HALF = P * PACK
 HALVES = H // HALF
 TILES = H // P
-QUARTER = PN // 4
-AHEAD = 2
-RING = 2
-PICKS = 4
-LAG = 0
-WO_STEP = 1
-LAST_TAG = "h1"
+LAST = TILES - 1
+CHUNKS = S // P
+QUADRANTS = 4
+PER_COLUMN = 16
+RUN = 4
+QUARTERS = 4
+QUARTER = PN // QUARTERS
 ADD_ON_VECTOR = 5
-EARLY = 6
-SINE_ORDER = list(range(TILES))
-LOADS = "tab p1 a0 p2 p3 a1 p4 p5 wg o0 p6 o1 p7"
-WO0 = 0
+AHEAD = 2
 
 
 def tile_list_embankment_slot_board_kernel(
@@ -53,17 +50,20 @@ def tile_list_embankment_slot_board_kernel(
         def bank(name, index):
             return psum.tile([P, HALF], F32, name=name, tag="bank%d" % index)
 
+        def entries(offsets, j0, j1):
+            return offsets[:, j0 // PER_COLUMN : j1 // PER_COLUMN]
+
         def load_list(name, src):
             dst = lists.tile(list(src.shape), U16, name=name, tag=name)
             nc.sync.dma_start(dst[:], src)
             return dst
 
-        def load_words(name, src, tag, bufs):
+        def load_words(name, src, tag, bufs=1):
             dst = sbuf(name, [P, src.shape[2]], I32, tag=tag, bufs=bufs)
             nc.sync.dma_start(dst[:], src[0].rearrange("p n i -> p (n i)").bitcast(I32))
             return dst
 
-        def zeroed_plane(name, src):
+        def zeroed_planes(name, src):
             dst = sbuf(name, [P, src.shape[0], src.shape[2]], U8)
             nc.vector.memset(dst[:].bitcast(I32), 0)
             return dst
@@ -71,29 +71,17 @@ def tile_list_embankment_slot_board_kernel(
         def load_scales(dst, src):
             words = dst[:].bitcast(I32)
             rows = src.bitcast(I32).rearrange("a r n -> r a n")
-            for q in range(4):
+            for q in range(QUADRANTS):
                 nc.sync.dma_start(words[32 * q : 32 * q + 4, :, :], rows[4 * q : 4 * q + 4, :, :])
 
-        def load_dealt(dst, src, t0, t1, queue):
-            rows = src.rearrange("(p t) j -> p t j", t=PACK)
-            for q in range(4):
-                queue.dma_start(dst[32 * q : 32 * (q + 1), t0:t1, :], rows[:, t0:t1, :])
-
-        def rows_of(src, i):
-            return src.rearrange("(b p t) c -> b t p c", b=HALVES, t=PACK)[i // PACK, i % PACK, :, :]
-
-        def load_page(i):
-            dst = sbuf("page%d" % i, [P, T2], F32)
-            nc.sync.dma_start(dst[:], rows_of(page0, i))
+        def load_dealt(name, src, tag, queue):
+            dst = sbuf(name, [P, PACK, S], F32, tag=tag)
+            for q in (0, 2, 1, 3):
+                queue.dma_start(dst[32 * q : 32 * (q + 1), :, :], src.rearrange("(p t) j -> p t j", t=PACK))
             return dst
 
-        def load_base(i):
-            dst = sbuf("base%d" % i, [P, S], F32, tag="base", bufs=4)
-            nc.sync.dma_start(dst[:], rows_of(base, i))
-            return dst
-
-        def load_raw(name, src, tag, bufs):
-            dst = sbuf(name, [P, PACK, HALF], F32, tag=tag, bufs=bufs)
+        def load_rows(name, src, tag):
+            dst = sbuf(name, [P, PACK, HALF], F32, tag=tag)
             nc.sync.dma_start(dst[:], src.rearrange("(p j) c -> p j c", j=PACK))
             return dst
 
@@ -102,89 +90,87 @@ def tile_list_embankment_slot_board_kernel(
             nc.sync.dma_start(dst[:], src.rearrange("(b p t) -> p b t", b=HALVES, t=PACK))
             return dst
 
+        pages, bases = [], []
+
+        def load_tile(i):
+            for tiles, name, src, tag, bufs in ((pages, "page", page0, "page%d" % i, 1), (bases, "base", base, "base", 4)):
+                tiles.append(sbuf("%s%d" % (name, i), [P, src.shape[1]], F32, tag=tag, bufs=bufs))
+                rows = src.rearrange("(b p t) c -> b t p c", b=HALVES, t=PACK)
+                nc.sync.dma_start(tiles[i][:], rows[i // PACK, i % PACK, :, :])
+
         def woven(name):
             return sbuf(name, [P, PACK * HALF], BF16, tag="woven", bufs=3)
 
-        def quantize(codes, scales, src):
-            nc.vector.quantize_mx(out=codes.bitcast(FP8X4), scales=scales, in_=src)
+        def quantize(codes, plane, src):
+            nc.vector.quantize_mx(out=codes.bitcast(FP8X4), scales=plane, in_=src)
 
-        def mx(dst, lhs, lhs_scale, rhs, rhs_scale, start, stop, lhs_dtype=FP8X4):
-            nc.tensor.matmul_mx(
-                out=dst, lhsT=lhs.bitcast(lhs_dtype), lhsT_scale=lhs_scale,
-                rhs=rhs.bitcast(FP8X4), rhs_scale=rhs_scale, start=start, stop=stop,
-            )
-
-        def pick_table(name, words, scales, idx, pieces):
-            codes = sbuf(name + "_codes", [P, S], U32)
-            plane = sbuf(name + "_plane", [P, S], U8)
-            n = S // pieces
-            for j in range(0, S, n):
-                entries = idx[:, j // 16 : (j + n) // 16]
-                nc.vector.tensor_copy(codes[:, j : j + n], words[:].bitcast(U32).indirect(entries))
-                nc.vector.tensor_copy(plane[:, j : j + n], scales[:, 0, :].indirect(entries))
+        def quantize_pass(name, src):
+            codes = sbuf(name + "_codes", [P, HALF], U32)
+            plane = sbuf(name + "_plane", [P, HALF], U8)
+            quantize(codes[:], plane[:], src[:])
             return codes, plane
 
-        tab2_sc = zeroed_plane("tab2_sc", tab2_scales)
-        w3_sc = zeroed_plane("w3_sc", w3_scales)
-        w2_sc = zeroed_plane("w2_sc", w2_scales)
-        tab_sc = zeroed_plane("tab_sc", tab_scales)
+        def mx(dst, lhs, lhs_plane, rhs, rhs_plane, start, stop, lhs_dtype=FP8X4):
+            nc.tensor.matmul_mx(
+                out=dst, lhsT=lhs.bitcast(lhs_dtype), lhsT_scale=lhs_plane,
+                rhs=rhs.bitcast(FP8X4), rhs_scale=rhs_plane, start=start, stop=stop,
+            )
+
+        tab2_sc = zeroed_planes("tab2_sc", tab2_scales)
+        w3_sc = zeroed_planes("w3_sc", w3_scales)
+        w2_sc = zeroed_planes("w2_sc", w2_scales)
+        tab_sc = zeroed_planes("tab_sc", tab_scales)
         minus_quarter = sbuf("minus_quarter", [P, 1], F32)
         nc.vector.memset(minus_quarter[:], -0.25)
         warm = sbuf("warm", [P, 1], F32)
         nc.scalar.activation(out=warm[:], in_=minus_quarter[:], func=ACT.Silu)
-
-        wg2_sb = sbuf("wg2_sb", [P, PACK, S], F32)
         ident = sbuf("ident", [P, P], F32)
         make_identity(nc, ident[:])
-        load_dealt(wg2_sb, wg2, 1, PACK, nc.gpsimd)
+
         idx2 = load_list("idx2", offs2)
-        tab2_sb = load_words("tab2_sb", tab2_words, "wide0", 1)
+        wg2_sb = load_dealt("wg2_sb", wg2, "wg2", nc.scalar)
+        tab2_sb = load_words("tab2_sb", tab2_words, "wide0")
         load_scales(tab2_sc, tab2_scales)
         w3_sb = load_words("w3_sb", w3_words, "codes", 2)
         load_scales(w3_sc, w3_scales)
         w2_sb = sbuf("w2_sb", [P, HALVES, H // 2], I32, tag="codes", bufs=2)
         nc.sync.dma_start(w2_sb[:], w2_words.bitcast(I32).rearrange("a p n -> p a n"))
         load_scales(w2_sc, w2_scales)
-        bases, pages, w1_raw, wo_raw = {}, {}, [], []
-
-        def load_tile(i):
-            pages[i] = load_page(i)
-            bases[i] = load_base(i)
-
-        def load_w1(b):
-            w1_raw.append(load_raw("w1_raw%d" % b, w1[:, b * HALF : (b + 1) * HALF], "stage%d" % (b + 1), 1))
-
-        def load_wo(b):
-            wo_raw.append(load_raw("wo_raw%d" % b, wo[b * HALF : (b + 1) * HALF, :], "wide%d" % b, 1))
-
         idx4 = load_list("idx4", offs4)
-        bases[0] = load_base(0)
-        load_dealt(wg2_sb, wg2, 0, 1, nc.sync)
-        pages[0] = load_page(0)
-        for item in LOADS.split():
-            if item == "tab":
-                tab_sb = load_words("tab_sb", tab_words, "tab", 1)
-                idx = load_list("idx", offs)
-                load_scales(tab_sc, tab_scales)
-            if item[0] == "p":
-                load_tile(int(item[1]))
-            if item[0] == "a":
-                load_w1(int(item[1]))
-            if item == "a0":
-                gt_sb = load_gain("gt_sb", gt)
-                gx_sb = load_gain("gx_sb", gx)
-            if item[0] == "o":
-                load_wo(int(item[1]))
-            if item == "wg":
-                idx3 = load_list("idx3", offs3)
-                idx5 = load_list("idx5", offs5)
+        load_tile(0)
+        gx_sb = load_gain("gx_sb", gx)
+        tab_sb = load_words("tab_sb", tab_words, "tab")
+        idx = load_list("idx", offs)
+        load_scales(tab_sc, tab_scales)
+        load_tile(1)
+        w1_rows = [load_rows("w1_rows0", w1[:, :HALF], "stage1")]
+        gt_sb = load_gain("gt_sb", gt)
+        load_tile(2)
+        load_tile(3)
+        w1_rows.append(load_rows("w1_rows1", w1[:, HALF:], "stage2"))
+        load_tile(4)
+        load_tile(5)
+        idx3 = load_list("idx3", offs3)
+        idx5 = load_list("idx5", offs5)
+        wg1_sb = load_dealt("wg1_sb", wg1, "tab", nc.sync)
+        wo_rows = [load_rows("wo_rows0", wo[:HALF, :], "wide0")]
+        load_tile(6)
+        wo_rows.append(load_rows("wo_rows1", wo[HALF:, :], "wide1"))
+        load_tile(7)
 
-        v2_codes, v2_plane = pick_table("v2", tab2_sb, tab2_sc, idx2, 2)
+        def pick_table(name, words, planes, offsets, pieces):
+            codes = sbuf(name + "_codes", [P, S], U32)
+            plane = sbuf(name + "_plane", [P, S], U8)
+            n = S // pieces
+            for j in range(0, S, n):
+                nc.vector.tensor_copy(codes[:, j : j + n], words[:].bitcast(U32).indirect(entries(offsets, j, j + n)))
+                nc.vector.tensor_copy(plane[:, j : j + n], planes[:, 0, :].indirect(entries(offsets, j, j + n)))
+            return codes, plane
 
-        turns = [sbuf("turns%d" % b, [P, PACK, PACK, P], F32, tag="stage%d" % b) for b in range(HALVES)]
+        turns = [sbuf("turns%d" % b, [P, PACK, CHUNKS, P], F32, tag="stage%d" % b) for b in range(HALVES)]
 
-        def turns_of_chunk(b, c):
-            z = bank("z%d_%d" % (b, c), 4 + c if b == 0 else 6 + c % 2)
+        def turns_of_chunk(b, c, bank_index):
+            z = bank("z%d_%d" % (b, c), bank_index)
             js = slice(c * P, (c + 1) * P)
             rs = slice(b * HALF, (b + 1) * HALF)
             mx(z[:], v2_codes[:, js], v2_plane[:, js], w3_sb[:, rs], w3_sc[:, 0, rs], True, True)
@@ -199,215 +185,209 @@ def tile_list_embankment_slot_board_kernel(
                 nc.tensor.matmul(dst[:, js], lhsT=left[:, js], rhs=ident[:], is_transpose=True, start=True, stop=False)
                 nc.tensor.matmul(dst[:, js], lhsT=right[:, js], rhs=ident[:], is_transpose=True, start=False, stop=True)
 
-        def sine_tile(step, pieces=1):
-            i = SINE_ORDER[step]
-            mine = turns[i // PACK][:, i % PACK, :, :].rearrange("p c q -> p (c q)")
+        def sine_tiles(i):
             whole = sbuf("whole%d" % i, [P, S], U32, tag="whole", bufs=2)
             shift = sbuf("shift%d" % i, [P, S], F32, tag="shift", bufs=2)
             sine = sbuf("sine%d" % i, [P, S], F32, tag="sine", bufs=2)
-            n = S // pieces
-            for j in range(0, S, n):
-                js = slice(j, j + n)
-                if pieces > 1:
-                    h2 = sbuf("h2_%d_%d" % (i, j), [P, n], F32, tag="h2_piece")
-                else:
-                    h2 = sbuf("h2_%d" % i, [P, S], F32, tag="h2", bufs=4)
-                if step == 0:
-                    for c in range(j // P, (j + n) // P):
-                        turns_of_chunk(0, c)
-                nc.scalar.activation(out=whole[:, js], in_=mine[:, js], func=ACT.Copy, scale=1.0, bias=0.25)
-                nc.scalar.activation(out=shift[:, js], in_=whole[:, js], func=ACT.Copy, scale=-1.0, bias=0.25)
-                rest = bank("rest%d_%d" % (i, j), 4 + (step + j // n) % 2)
-                add_turned(rest, mine, shift, j, j + n)
-                nc.scalar.activation(out=sine[:, js], in_=rest[:, js], func=ACT.Sin, scale=2.0 * math.pi)
-                if step < ADD_ON_VECTOR:
-                    nc.vector.tensor_tensor(h2[:], sine[:, js], bases[i][:, js], ALU.add)
-                else:
-                    turned = bank("turned%d" % i, 6)
-                    add_turned(turned, sine, bases[i], 0, S)
-                    h2_turned = sbuf("h2_turned%d" % i, [P, S], F32, tag="h2_turned", bufs=2)
-                    nc.scalar.copy(out=h2_turned[:], in_=turned[:])
-                    back = bank("back%d" % i, 7)
-                    for c in range(PACK):
-                        cs = slice(c * P, (c + 1) * P)
-                        nc.tensor.transpose(back[:, cs], h2_turned[:, cs], ident[:])
-                    nc.scalar.copy(out=h2[:], in_=back[:])
-                entries = idx4[:, j // 16 : (j + n) // 16]
-                nc.vector.tensor_tensor(pages[i][:].indirect(entries), h2[:], wg2_sb[:, i % PACK, js], ALU.mult)
+            return whole, shift, sine
+
+        def sine_of(i, j0, j1, whole, shift, sine, bank_index):
+            js = slice(j0, j1)
+            u = turns[i // PACK][:, i % PACK, :, :].rearrange("p c q -> p (c q)")
+            nc.scalar.activation(out=whole[:, js], in_=u[:, js], func=ACT.Copy, scale=1.0, bias=0.25)
+            nc.scalar.activation(out=shift[:, js], in_=whole[:, js], func=ACT.Copy, scale=-1.0, bias=0.25)
+            rest = bank("rest%d_%d" % (i, j0), bank_index)
+            add_turned(rest, u, shift, j0, j1)
+            nc.scalar.activation(out=sine[:, js], in_=rest[:, js], func=ACT.Sin, scale=2.0 * math.pi)
+
+        def put_h2(i, j0, j1, h2):
+            nc.vector.tensor_tensor(
+                pages[i][:].indirect(entries(idx4, j0, j1)), h2[:], wg2_sb[:, i % PACK, j0:j1], ALU.mult
+            )
+
+        def place_h2(i):
+            h2 = sbuf("h2_%d" % i, [P, S], F32, tag="h2", bufs=4)
+            whole, shift, sine = sine_tiles(i)
+            sine_of(i, 0, S, whole, shift, sine, 4 + i % 2)
+            if i < ADD_ON_VECTOR:
+                nc.vector.tensor_tensor(h2[:], sine[:], bases[i][:], ALU.add)
+            else:
+                turned = bank("turned%d" % i, 6)
+                add_turned(turned, sine, bases[i], 0, S)
+                h2_turned = sbuf("h2_turned%d" % i, [P, S], F32, tag="h2_turned", bufs=2)
+                nc.scalar.copy(out=h2_turned[:], in_=turned[:])
+                back = bank("back%d" % i, 7)
+                for c in range(CHUNKS):
+                    js = slice(c * P, (c + 1) * P)
+                    nc.tensor.transpose(back[:, js], h2_turned[:, js], ident[:])
+                nc.scalar.copy(out=h2[:], in_=back[:])
+            put_h2(i, 0, S, h2)
+
+        v2_codes, v2_plane = pick_table("v2", tab2_sb, tab2_sc, idx2, 2)
 
         w2_codes = sbuf("w2_codes", [P, HALVES, 2 * H], U8)
         w2_plane = sbuf("w2_plane", [P, HALVES, H], U8)
         nc.vector.tensor_copy(
-            w2_codes[:].bitcast(U16).rearrange("p a (b t q) -> p (a b) q t", b=HALVES, t=PACK),
-            w2_sb[:].bitcast(U16).rearrange("p a (b q t) -> p (a b) q t", b=HALVES, t=PACK),
+            w2_codes[:].bitcast(U16).rearrange("p a (b t q) -> p (a b) t q", b=HALVES, t=PACK),
+            w2_sb[:].bitcast(U16).rearrange("p a (b q t) -> p (a b) t q", b=HALVES, t=PACK),
         )
         nc.vector.tensor_copy(
-            w2_plane[:].rearrange("p a (b t q) -> p (a b) q t", b=HALVES, t=PACK),
-            w2_sc[:].rearrange("p a (b q t) -> p (a b) q t", b=HALVES, t=PACK),
+            w2_plane[:].rearrange("p a (b t q) -> p (a b) t q", b=HALVES, t=PACK),
+            w2_sc[:].rearrange("p a (b q t) -> p (a b) t q", b=HALVES, t=PACK),
         )
 
-        sine_tile(0, 2)
-        v_codes, v_plane = pick_table("v", tab_sb, tab_sc, idx, 1)
-        wg1_sb = sbuf("wg1_sb", [P, PACK, S], F32, tag="tab")
-        load_dealt(wg1_sb, wg1, 0, PACK, nc.gpsimd)
+        first_tiles = sine_tiles(0)
+        for piece in range(2):
+            j0, j1 = piece * S // 2, (piece + 1) * S // 2
+            h2_piece = sbuf("h2_piece%d" % piece, [P, S // 2], F32, tag="h2_piece")
+            for c in range(j0 // P, j1 // P):
+                turns_of_chunk(0, c, 4 + c)
+            sine_of(0, j0, j1, *first_tiles, 4 + piece)
+            nc.vector.tensor_tensor(h2_piece[:], first_tiles[2][:, j0:j1], bases[0][:, j0:j1], ALU.add)
+            put_h2(0, j0, j1, h2_piece)
+
         gx_sign = sbuf("gx_sign", [P, HALVES, PACK], F32)
-        nc.gpsimd.tensor_scalar(gx_sign[:], gx_sb[:], 0.0, 2.0, ALU.is_ge, ALU.mult)
-        nc.gpsimd.tensor_scalar(gx_sign[:], gx_sign[:], 1.0, -1.0, ALU.mult, ALU.add)
+        nc.vector.tensor_scalar(gx_sign[:], gx_sb[:], 0.0, 2.0, ALU.is_ge, ALU.mult)
+        nc.vector.tensor_scalar(gx_sign[:], gx_sign[:], 1.0, -1.0, ALU.mult, ALU.add)
+        v_codes, v_plane = pick_table("v", tab_sb, tab_sc, idx, 1)
+        place_h2(1)
 
-        sine_tile(1)
-        sine_tile(2)
-
-        w1_codes, w1_plane, t_codes, t_plane = [], [], [], []
+        w1_q, t_q = [], []
         for b in range(HALVES):
-            grouped = woven("w1_woven%d" % b)
+            w1_woven = woven("w1_woven%d" % b)
             nc.scalar.copy(
-                out=grouped[:].rearrange("p (t m j) -> p m j t", t=PACK, j=PACK),
-                in_=w1_raw[b][:].rearrange("p j (m t) -> p m j t", t=PACK),
+                out=w1_woven[:].rearrange("p (t m j) -> p m t j", t=PACK, j=PACK),
+                in_=w1_rows[b][:].rearrange("p j (m t) -> p m t j", t=PACK),
             )
-            w1_codes.append(sbuf("w1_codes%d" % b, [P, HALF], U32))
-            w1_plane.append(sbuf("w1_plane%d" % b, [P, HALF], U8))
-            quantize(w1_codes[b][:], w1_plane[b][:], grouped[:])
+            w1_q.append(quantize_pass("w1_%d" % b, w1_woven))
             if b == 1:
-                for c in range(PACK):
-                    turns_of_chunk(1, c)
-            sine_tile(3 + b)
+                for c in range(CHUNKS):
+                    turns_of_chunk(1, c, 6 + c % 2)
+            place_h2(2 + 2 * b)
             tanh_y = sbuf("tanh_y%d" % b, [P, S, PACK], F32, tag="stage%d" % (2 * b))
-            for c in range(PACK):
+            for c in range(CHUNKS):
                 y = bank("y%d_%d" % (b, c), c)
                 js = slice(c * P, (c + 1) * P)
                 for t in range(PACK):
-                    ts = slice(t * P, (t + 1) * P)
-                    mx(y[:, ts], w1_codes[b][:, ts], w1_plane[b][:, ts], v_codes[:, js], v_plane[:, js], True, True)
+                    ms = slice(t * P, (t + 1) * P)
+                    mx(y[:, ms], w1_q[b][0][:, ms], w1_q[b][1][:, ms], v_codes[:, js], v_plane[:, js], True, True)
                 nc.scalar.activation(out=tanh_y[:, js, :], in_=y[:].rearrange("p (t j) -> p j t", t=PACK), func=ACT.Tanh)
-            grouped = woven("t_woven%d" % b)
+            t_woven = woven("t_woven%d" % b)
             nc.vector.tensor_tensor(
-                grouped[:].rearrange("p (j t) -> p j t", t=PACK),
+                t_woven[:].rearrange("p (j t) -> p j t", t=PACK),
                 tanh_y[:], gt_sb[:, b : b + 1, :].to_broadcast([P, S, PACK]), ALU.mult,
             )
-            t_codes.append(sbuf("t_codes%d" % b, [P, S], U32))
-            t_plane.append(sbuf("t_plane%d" % b, [P, S], U8))
-            quantize(t_codes[b][:], t_plane[b][:], grouped[:])
-        for step in range(5, EARLY):
-            sine_tile(step)
+            t_q.append(quantize_pass("t_%d" % b, t_woven))
+            place_h2(3 + 2 * b)
+        h2_placed = 2 + 2 * HALVES
 
-        def thermistor_tile(i):
-            b, ts = i // PACK, slice((i % PACK) * P, (i % PACK + 1) * P)
+        def place_h1(i):
+            w1_codes, w1_plane = w1_q[i // PACK]
+            ms = slice((i % PACK) * P, (i % PACK + 1) * P)
             acc = bank("h1_acc%d" % i, i % PACK)
             for a in reversed(range(HALVES)):
                 mx(
                     acc[:], w2_codes[:, a, 2 * P * i : 2 * P * (i + 1)], w2_plane[:, a, P * i : P * (i + 1)],
-                    t_codes[a][:], t_plane[a][:], a == HALVES - 1, False, lhs_dtype=FP4X4,
+                    t_q[a][0][:], t_q[a][1][:], a == HALVES - 1, False, lhs_dtype=FP4X4,
                 )
-            mx(acc[:], w1_codes[b][:, ts], w1_plane[b][:, ts], v_codes[:], v_plane[:], False, True)
-            h1 = sbuf("h1_%d" % i, [P, S], F32, tag="h1", bufs=4) if i < TILES - 1 or LAST_TAG == "h1" else sbuf("h1_%d" % i, [P, S], F32, tag="woven", bufs=3)
+            mx(acc[:], w1_codes[:, ms], w1_plane[:, ms], v_codes[:], v_plane[:], False, True)
+            h1 = sbuf("h1_%d" % i, [P, S], F32, tag="h1", bufs=4)
             nc.scalar.copy(out=h1[:], in_=acc[:])
-            return h1
+            nc.vector.tensor_tensor(pages[i][:].indirect(idx3[:]), h1[:], wg1_sb[:, i % PACK, :], ALU.mult)
 
         x_rows = [sbuf("x_rows%d" % b, [P, PACK, PN], BF16, tag="wide%d" % b) for b in range(HALVES)]
         x_codes = [sbuf("x_codes%d" % b, [P, PN], U32, tag="codes", bufs=2) for b in range(HALVES)]
         x_plane = [sbuf("x_plane%d" % b, [P, PN], U8) for b in range(HALVES)]
+        x_last_woven = sbuf("x_last_woven", [P, PN, PACK], BF16, tag="stage2")
 
-        def place(i):
-            h1 = thermistor_tile(i)
-            nc.vector.tensor_tensor(pages[i][:].indirect(idx3[:]), h1[:], wg1_sb[:, i % PACK, :], ALU.mult)
-
-        def pick(i, j0, j1, tag, bufs=2):
+        def read_slots(i, j0, j1, tag, bufs):
             picked = sbuf("picked%d_%d" % (i, j0), [P, j1 - j0], F32, tag=tag, bufs=bufs)
-            nc.vector.tensor_copy(picked[:], pages[i][:].indirect(idx5[:, j0 // 16 : j1 // 16]))
+            nc.vector.tensor_copy(picked[:], pages[i][:].indirect(entries(idx5, j0, j1)))
             return picked
 
         def gain_slots(i, j0, j1, picked):
             b, t = i // PACK, i % PACK
             nc.scalar.activation(out=x_rows[b][:, t, j0:j1], in_=picked[:], func=ACT.Abs, scale=gx_sb[:, b, t : t + 1])
 
-        def weave_pair(u, j0, j1, copy):
+        def quantize_first_x():
+            for j in range(0, PN, HALF):
+                x_woven = woven("x_woven%d" % j)
+                nc.scalar.copy(
+                    out=x_woven[:].rearrange("p (c i t) -> p c t i", i=RUN, t=PACK),
+                    in_=x_rows[0][:, :, j : j + HALF].rearrange("p t (c i) -> p c t i", i=RUN),
+                )
+                quantize(x_codes[0][:, j : j + HALF], x_plane[0][:, j : j + HALF], x_woven[:])
+
+        def weave_pair(copy, t0, j0, j1):
             copy(
-                last_woven[:, j0:j1, 2 * u : 2 * u + 2].rearrange("p (c i) t -> p c t i", i=4),
-                x_rows[1][:, 2 * u : 2 * u + 2, j0:j1].rearrange("p t (c i) -> p c t i", i=4),
+                x_last_woven[:, j0:j1, t0 : t0 + 2].rearrange("p (c i) t -> p c t i", i=RUN),
+                x_rows[1][:, t0 : t0 + 2, j0:j1].rearrange("p t (c i) -> p c t i", i=RUN),
             )
-
-        def quantize_x(b, j0, j1, copy):
-            grouped = woven("x_woven%d_%d" % (b, j0))[:, 0 : PACK * (j1 - j0)]
-            copy(
-                grouped.rearrange("p (c i t) -> p c t i", i=4, t=PACK),
-                x_rows[b][:, :, j0:j1].rearrange("p t (c i) -> p c t i", i=4),
-            )
-            quantize(x_codes[b][:, j0:j1], x_plane[b][:, j0:j1], grouped)
-
-        last_woven = sbuf("last_woven", [P, PN, PACK], BF16, tag="stage2")
-
-        wo_codes, wo_plane = [], []
 
         def quantize_wo(b):
-            wo_rows = woven("wo_rows%d" % b)
+            wo_signed = woven("wo_signed%d" % b)
             for t in range(PACK):
                 nc.scalar.activation(
-                    out=wo_rows[:, t * N : (t + 1) * N], in_=wo_raw[b][:, t, :], func=ACT.Copy,
+                    out=wo_signed[:, t * N : (t + 1) * N], in_=wo_rows[b][:, t, :], func=ACT.Copy,
                     scale=gx_sign[:, b, t : t + 1],
                 )
-            grouped = woven("wo_woven%d" % b)
+            wo_woven = woven("wo_woven%d" % b)
             nc.scalar.copy(
-                out=grouped[:].rearrange("p (c i j) -> p c j i", i=4, j=PACK),
-                in_=wo_rows[:].rearrange("p (j c i) -> p c j i", i=4, j=PACK),
+                out=wo_woven[:].rearrange("p (c i t) -> p c t i", i=RUN, t=PACK),
+                in_=wo_signed[:].rearrange("p (t c i) -> p c t i", i=RUN, t=PACK),
             )
-            wo_codes.append(sbuf("wo_codes%d" % b, [P, N], U32))
-            wo_plane.append(sbuf("wo_plane%d" % b, [P, N], U8))
-            quantize(wo_codes[b][:], wo_plane[b][:], grouped[:])
+            return quantize_pass("wo_%d" % b, wo_woven)
 
-        quantize_wo(0)
+        picks = []
         for i in range(AHEAD):
-            place(i)
-        picks = [pick(i, 0, PN, "picked", PICKS) for i in range(AHEAD - LAG)]
-        for i in range(TILES - 1):
-            if EARLY + i < TILES:
-                sine_tile(EARLY + i)
+            place_h1(i)
+            picks.append(read_slots(i, 0, PN, "picked", 4))
+        wo_q = [quantize_wo(0)]
+        for i in range(LAST):
+            if h2_placed + i < TILES:
+                place_h2(h2_placed + i)
             if i + AHEAD < TILES:
-                place(i + AHEAD)
-            if LAG:
-                gain_slots(i, 0, PN, picks[i])
-            if i + AHEAD - LAG < TILES - 1:
-                picks.append(pick(i + AHEAD - LAG, 0, PN, "picked", PICKS))
-            if not LAG:
-                gain_slots(i, 0, PN, picks[i])
+                place_h1(i + AHEAD)
+            if i + AHEAD < LAST:
+                picks.append(read_slots(i + AHEAD, 0, PN, "picked", 4))
+            gain_slots(i, 0, PN, picks[i])
+            if i == 0:
+                wo_q.append(quantize_wo(1))
             if i == PACK - 1:
-                for h in range(2):
-                    quantize_x(0, h * HALF, (h + 1) * HALF, nc.scalar.copy)
+                quantize_first_x()
             if i == PACK + 1:
-                weave_pair(0, 0, PN, nc.scalar.copy)
-            if i == WO_STEP:
-                quantize_wo(1)
+                weave_pair(nc.scalar.copy, 0, 0, PN)
 
         def score_pass(acc, b, pair, q):
+            wo_codes, wo_plane = wo_q[b]
             js = slice(q * QUARTER, (q + 1) * QUARTER)
-            for u in range(2):
-                ns = slice((2 * pair + u) * P, (2 * pair + u + 1) * P)
+            for side in range(2):
+                ns = slice((2 * pair + side) * P, (2 * pair + side + 1) * P)
                 mx(
-                    acc[:, u * QUARTER : (u + 1) * QUARTER], wo_codes[b][:, ns], wo_plane[b][:, ns],
-                    x_codes[b][:, js], x_plane[b][:, js], b == 0 and u == 0, b == 1 and u == 1,
+                    acc[:, side * QUARTER : (side + 1) * QUARTER], wo_codes[:, ns], wo_plane[:, ns],
+                    x_codes[b][:, js], x_plane[b][:, js], b == 0 and side == 0, b == 1 and side == 1,
                 )
 
         scores = {}
-        for q in range(4):
+        for q in range(QUARTERS):
             for pair in range(2):
-                scores[q, pair] = bank("score%d_%d" % (q, pair), (2 * q + pair + 4) % 8)
+                scores[q, pair] = bank("score%d_%d" % (q, pair), (4 + 2 * q + pair) % 8)
                 score_pass(scores[q, pair], 0, pair, q)
 
-        parts = [pick(TILES - 1, q * QUARTER, (q + 1) * QUARTER, "sine", RING) for q in range(RING)]
-        for q in range(4):
+        parts = [read_slots(LAST, q * QUARTER, (q + 1) * QUARTER, "sine", 2) for q in range(2)]
+        for q in range(QUARTERS):
             j0, j1 = q * QUARTER, (q + 1) * QUARTER
-            gain_slots(TILES - 1, j0, j1, parts[q])
-            weave_pair(1, j0, j1, nc.vector.tensor_copy)
-            quantize(x_codes[1][:, j0:j1], x_plane[1][:, j0:j1], last_woven[:, j0:j1, :].rearrange("p j t -> p (j t)"))
-            if q + RING < 4:
-                parts.append(pick(TILES - 1, j0 + RING * QUARTER, j1 + RING * QUARTER, "sine", RING))
-        for q in range(4):
-            j0, j1 = q * QUARTER, (q + 1) * QUARTER
+            gain_slots(LAST, j0, j1, parts[q])
+            weave_pair(nc.vector.tensor_copy, 2, j0, j1)
+            quantize(x_codes[1][:, j0:j1], x_plane[1][:, j0:j1], x_last_woven[:, j0:j1, :].rearrange("p j t -> p (j t)"))
+            if q + 2 < QUARTERS:
+                parts.append(read_slots(LAST, j0 + 2 * QUARTER, j1 + 2 * QUARTER, "sine", 2))
+        for q in range(QUARTERS):
             for pair in range(2):
                 score_pass(scores[q, pair], 1, pair, q)
                 result = sbuf("result%d_%d" % (q, pair), [P, 2, QUARTER], F32, tag="page%d" % (2 * q + pair))
                 nc.scalar.activation(
                     out=result[:].rearrange("p u j -> p (u j)"), in_=scores[q, pair][:], func=ACT.Tanh
                 )
-                nc.sync.dma_start(
-                    out[2 * pair * P : 2 * (pair + 1) * P, j0:j1].rearrange("(u p) j -> p u j", u=2), result[:]
-                )
+                rows = out[2 * pair * P : 2 * (pair + 1) * P, q * QUARTER : (q + 1) * QUARTER]
+                nc.sync.dma_start(rows.rearrange("(u p) j -> p u j", u=2), result[:])

@@ -70,9 +70,9 @@ def tile_list_embankment_slot_board_kernel(
 
         def load_scales(dst, src):
             words = dst[:].bitcast(I32)
-            rows = src.bitcast(I32).rearrange("a r n -> r a n")
-            for q in range(QUADRANTS):
-                nc.sync.dma_start(words[32 * q : 32 * q + 4, :, :], rows[4 * q : 4 * q + 4, :, :])
+            rows = src.bitcast(I32).rearrange("a (q s) n -> s q a n", q=QUADRANTS)
+            for s in range(4):
+                nc.sync.dma_start(words[s:P:32, :, :], rows[s, :, :, :])
 
         def load_dealt(name, src, tag, queue):
             dst = sbuf(name, [P, PACK, S], F32, tag=tag)
@@ -120,10 +120,12 @@ def tile_list_embankment_slot_board_kernel(
         w3_sc = zeroed_planes("w3_sc", w3_scales)
         w2_sc = zeroed_planes("w2_sc", w2_scales)
         tab_sc = zeroed_planes("tab_sc", tab_scales)
+        zero = sbuf("zero", [P, 1], F32)
+        nc.vector.memset(zero[:], 0.0)
+        silu_of_zero = sbuf("silu_of_zero", [P, 1], F32)
+        nc.scalar.activation(out=silu_of_zero[:], in_=zero[:], func=ACT.Silu)
         minus_quarter = sbuf("minus_quarter", [P, 1], F32)
-        nc.vector.memset(minus_quarter[:], -0.25)
-        warm = sbuf("warm", [P, 1], F32)
-        nc.scalar.activation(out=warm[:], in_=minus_quarter[:], func=ACT.Silu)
+        nc.vector.tensor_scalar(minus_quarter[:], silu_of_zero[:], -0.25, None, ALU.add)
         ident = sbuf("ident", [P, P], F32)
         make_identity(nc, ident[:])
 
@@ -319,10 +321,7 @@ def tile_list_embankment_slot_board_kernel(
                 quantize(x_codes[0][:, j : j + HALF], x_plane[0][:, j : j + HALF], x_woven[:])
 
         def weave_pair(copy, t0, j0, j1):
-            copy(
-                x_last_woven[:, j0:j1, t0 : t0 + 2].rearrange("p (c i) t -> p c t i", i=RUN),
-                x_rows[1][:, t0 : t0 + 2, j0:j1].rearrange("p t (c i) -> p c t i", i=RUN),
-            )
+            copy(x_last_woven[:, j0:j1, t0 : t0 + 2], x_rows[1][:, t0 : t0 + 2, j0:j1].rearrange("p t j -> p j t"))
 
         def quantize_wo(b):
             wo_signed = woven("wo_signed%d" % b)
@@ -374,15 +373,7 @@ def tile_list_embankment_slot_board_kernel(
                 scores[q, pair] = bank("score%d_%d" % (q, pair), (4 + 2 * q + pair) % 8)
                 score_pass(scores[q, pair], 0, pair, q)
 
-        parts = [read_slots(LAST, q * QUARTER, (q + 1) * QUARTER, "sine", 2) for q in range(2)]
-        for q in range(QUARTERS):
-            j0, j1 = q * QUARTER, (q + 1) * QUARTER
-            gain_slots(LAST, j0, j1, parts[q])
-            weave_pair(nc.vector.tensor_copy, 2, j0, j1)
-            quantize(x_codes[1][:, j0:j1], x_plane[1][:, j0:j1], x_last_woven[:, j0:j1, :].rearrange("p j t -> p (j t)"))
-            if q + 2 < QUARTERS:
-                parts.append(read_slots(LAST, j0 + 2 * QUARTER, j1 + 2 * QUARTER, "sine", 2))
-        for q in range(QUARTERS):
+        def finish(q):
             for pair in range(2):
                 score_pass(scores[q, pair], 1, pair, q)
                 result = sbuf("result%d_%d" % (q, pair), [P, 2, QUARTER], F32, tag="page%d" % (2 * q + pair))
@@ -391,3 +382,17 @@ def tile_list_embankment_slot_board_kernel(
                 )
                 rows = out[2 * pair * P : 2 * (pair + 1) * P, q * QUARTER : (q + 1) * QUARTER]
                 nc.sync.dma_start(rows.rearrange("(u p) j -> p u j", u=2), result[:])
+
+        parts = [read_slots(LAST, q * QUARTER, (q + 1) * QUARTER, "sine", 2) for q in range(2)]
+        gain_slots(LAST, 0, QUARTER, parts[0])
+        for q in range(QUARTERS):
+            j0, j1 = q * QUARTER, (q + 1) * QUARTER
+            if q + 1 < QUARTERS:
+                gain_slots(LAST, j1, j1 + QUARTER, parts[q + 1])
+            weave_pair(nc.vector.tensor_copy, 2, j0, j1)
+            quantize(x_codes[1][:, j0:j1], x_plane[1][:, j0:j1], x_last_woven[:, j0:j1, :].rearrange("p j t -> p (j t)"))
+            if q + 2 < QUARTERS:
+                parts.append(read_slots(LAST, j0 + 2 * QUARTER, j1 + 2 * QUARTER, "sine", 2))
+            if q >= 1:
+                finish(q - 1)
+        finish(QUARTERS - 1)

import math
from contextlib import ExitStack

import concourse.mybir as mybir
from concourse.masks import make_identity

K, S, H, T2, PN, N = 512, 512, 1024, 2048, 1024, 512
FLOPS = 2 * (3 * K * H * S + H * H * S + H * N * PN)

F32 = mybir.dt.float32
BF16 = mybir.dt.bfloat16
I32 = mybir.dt.int32
U32 = mybir.dt.uint32
U16 = mybir.dt.uint16
U8 = mybir.dt.uint8
FP8X4 = mybir.dt.float8_e4m3fn_x4
FP4X4 = mybir.dt.float4_e2m1fn_x4
ACT = mybir.ActivationFunctionType
ALU = mybir.AluOpType

P = 128
PACK = 4
HALF = P * PACK
HALVES = H // HALF
TILES = H // P
LAST = TILES - 1
CHUNKS = S // P
QUADRANTS = 4
PER_COLUMN = 16
RUN = 4
QUARTERS = 4
QUARTER = PN // QUARTERS
ADD_ON_VECTOR = 5
AHEAD = 2


def tile_list_embankment_slot_board_kernel(
    tc, tab_words, tab_scales, offs, tab2_words, tab2_scales, offs2, w1, gt, w2_words, w2_scales,
    w3_words, w3_scales, base, page0, offs3, offs4, wg1, wg2, offs5, gx, wo, out,
):
    nc = tc.nc
    with ExitStack() as ctx:
        lists = ctx.enter_context(tc.tile_pool(name="lists", bufs=1))
        sb = ctx.enter_context(tc.tile_pool(name="sb", bufs=1))
        psum = ctx.enter_context(tc.psum_pool(name="psum", bufs=1))

        def sbuf(name, shape, dtype, tag=None, bufs=1):
            return sb.tile(shape, dtype, name=name, tag=tag or name, bufs=bufs, align_bytes=64)

        def bank(name, index):
            return psum.tile([P, HALF], F32, name=name, tag="bank%d" % index)

        def entries(offsets, j0, j1):
            return offsets[:, j0 // PER_COLUMN : j1 // PER_COLUMN]

        def load_list(name, src):
            dst = lists.tile(list(src.shape), U16, name=name, tag=name)
            nc.sync.dma_start(dst[:], src)
            return dst

        def load_words(name, src, tag, bufs=1):
            dst = sbuf(name, [P, src.shape[2]], I32, tag=tag, bufs=bufs)
            nc.sync.dma_start(dst[:], src[0].rearrange("p n i -> p (n i)").bitcast(I32))
            return dst

        def zeroed_planes(name, src):
            dst = sbuf(name, [P, src.shape[0], src.shape[2]], U8)
            nc.vector.memset(dst[:].bitcast(I32), 0)
            return dst

        def load_scales(dst, src):
            words = dst[:].bitcast(I32)
            rows = src.bitcast(I32).rearrange("a (q s) n -> s q a n", q=QUADRANTS)
            for s in range(4):
                nc.sync.dma_start(words[s:P:32, :, :], rows[s, :, :, :])

        def load_dealt(name, src, tag, queue):
            dst = sbuf(name, [P, PACK, S], F32, tag=tag)
            for q in (0, 2, 1, 3):
                queue.dma_start(dst[32 * q : 32 * (q + 1), :, :], src.rearrange("(p t) j -> p t j", t=PACK))
            return dst

        def load_rows(name, src, tag):
            dst = sbuf(name, [P, PACK, HALF], F32, tag=tag)
            nc.sync.dma_start(dst[:], src.rearrange("(p j) c -> p j c", j=PACK))
            return dst

        def load_gain(name, src):
            dst = sbuf(name, [P, HALVES, PACK], F32)
            nc.sync.dma_start(dst[:], src.rearrange("(b p t) -> p b t", b=HALVES, t=PACK))
            return dst

        pages, bases = [], []

        def load_tile(i):
            for tiles, name, src, tag, bufs in ((pages, "page", page0, "page%d" % i, 1), (bases, "base", base, "base", 4)):
                tiles.append(sbuf("%s%d" % (name, i), [P, src.shape[1]], F32, tag=tag, bufs=bufs))
                rows = src.rearrange("(b p t) c -> b t p c", b=HALVES, t=PACK)
                nc.sync.dma_start(tiles[i][:], rows[i // PACK, i % PACK, :, :])

        def woven(name):
            return sbuf(name, [P, PACK * HALF], BF16, tag="woven", bufs=3)

        def quantize(codes, plane, src):
            nc.vector.quantize_mx(out=codes.bitcast(FP8X4), scales=plane, in_=src)

        def quantize_pass(name, src):
            codes = sbuf(name + "_codes", [P, HALF], U32)
            plane = sbuf(name + "_plane", [P, HALF], U8)
            quantize(codes[:], plane[:], src[:])
            return codes, plane

        def mx(dst, lhs, lhs_plane, rhs, rhs_plane, start, stop, lhs_dtype=FP8X4):
            nc.tensor.matmul_mx(
                out=dst, lhsT=lhs.bitcast(lhs_dtype), lhsT_scale=lhs_plane,
                rhs=rhs.bitcast(FP8X4), rhs_scale=rhs_plane, start=start, stop=stop,
            )

        tab2_sc = zeroed_planes("tab2_sc", tab2_scales)
        w3_sc = zeroed_planes("w3_sc", w3_scales)
        w2_sc = zeroed_planes("w2_sc", w2_scales)
        tab_sc = zeroed_planes("tab_sc", tab_scales)
        zero = sbuf("zero", [P, 1], F32)
        nc.vector.memset(zero[:], 0.0)
        silu_of_zero = sbuf("silu_of_zero", [P, 1], F32)
        nc.scalar.activation(out=silu_of_zero[:], in_=zero[:], func=ACT.Silu)
        minus_quarter = sbuf("minus_quarter", [P, 1], F32)
        nc.vector.tensor_scalar(minus_quarter[:], silu_of_zero[:], -0.25, None, ALU.add)
        ident = sbuf("ident", [P, P], F32)
        make_identity(nc, ident[:])

        idx2 = load_list("idx2", offs2)
        wg2_sb = load_dealt("wg2_sb", wg2, "wg2", nc.scalar)
        tab2_sb = load_words("tab2_sb", tab2_words, "wide0")
        load_scales(tab2_sc, tab2_scales)
        w3_sb = load_words("w3_sb", w3_words, "codes", 2)
        load_scales(w3_sc, w3_scales)
        w2_sb = sbuf("w2_sb", [P, HALVES, H // 2], I32, tag="codes", bufs=2)
        nc.sync.dma_start(w2_sb[:], w2_words.bitcast(I32).rearrange("a p n -> p a n"))
        load_scales(w2_sc, w2_scales)
        idx4 = load_list("idx4", offs4)
        load_tile(0)
        gx_sb = load_gain("gx_sb", gx)
        tab_sb = load_words("tab_sb", tab_words, "tab")
        idx = load_list("idx", offs)
        load_scales(tab_sc, tab_scales)
        load_tile(1)
        w1_rows = [load_rows("w1_rows0", w1[:, :HALF], "stage1")]
        gt_sb = load_gain("gt_sb", gt)
        load_tile(2)
        load_tile(3)
        w1_rows.append(load_rows("w1_rows1", w1[:, HALF:], "stage2"))
        load_tile(4)
        load_tile(5)
        idx3 = load_list("idx3", offs3)
        idx5 = load_list("idx5", offs5)
        wg1_sb = load_dealt("wg1_sb", wg1, "tab", nc.sync)
        wo_rows = [load_rows("wo_rows0", wo[:HALF, :], "wide0")]
        load_tile(6)
        wo_rows.append(load_rows("wo_rows1", wo[HALF:, :], "wide1"))
        load_tile(7)

        def pick_table(name, words, planes, offsets, pieces):
            codes = sbuf(name + "_codes", [P, S], U32)
            plane = sbuf(name + "_plane", [P, S], U8)
            n = S // pieces
            for j in range(0, S, n):
                nc.vector.tensor_copy(codes[:, j : j + n], words[:].bitcast(U32).indirect(entries(offsets, j, j + n)))
                nc.vector.tensor_copy(plane[:, j : j + n], planes[:, 0, :].indirect(entries(offsets, j, j + n)))
            return codes, plane

        turns = [sbuf("turns%d" % b, [P, PACK, CHUNKS, P], F32, tag="stage%d" % b) for b in range(HALVES)]

        def turns_of_chunk(b, c, bank_index):
            z = bank("z%d_%d" % (b, c), bank_index)
            js = slice(c * P, (c + 1) * P)
            rs = slice(b * HALF, (b + 1) * HALF)
            mx(z[:], v2_codes[:, js], v2_plane[:, js], w3_sb[:, rs], w3_sc[:, 0, rs], True, True)
            nc.scalar.activation(
                out=turns[b][:, :, c, :], in_=z[:].rearrange("p (q t) -> p t q", t=PACK),
                func=ACT.Abs, scale=1.0 / (2.0 * math.pi), bias=minus_quarter[:],
            )

        def add_turned(dst, left, right, j0, j1):
            for j in range(j0, j1, P):
                js = slice(j, j + P)
                nc.tensor.matmul(dst[:, js], lhsT=left[:, js], rhs=ident[:], is_transpose=True, start=True, stop=False)
                nc.tensor.matmul(dst[:, js], lhsT=right[:, js], rhs=ident[:], is_transpose=True, start=False, stop=True)

        def sine_tiles(i):
            whole = sbuf("whole%d" % i, [P, S], U32, tag="whole", bufs=2)
            shift = sbuf("shift%d" % i, [P, S], F32, tag="shift", bufs=2)
            sine = sbuf("sine%d" % i, [P, S], F32, tag="sine", bufs=2)
            return whole, shift, sine

        def sine_of(i, j0, j1, whole, shift, sine, bank_index):
            js = slice(j0, j1)
            u = turns[i // PACK][:, i % PACK, :, :].rearrange("p c q -> p (c q)")
            nc.scalar.activation(out=whole[:, js], in_=u[:, js], func=ACT.Copy, scale=1.0, bias=0.25)
            nc.scalar.activation(out=shift[:, js], in_=whole[:, js], func=ACT.Copy, scale=-1.0, bias=0.25)
            rest = bank("rest%d_%d" % (i, j0), bank_index)
            add_turned(rest, u, shift, j0, j1)
            nc.scalar.activation(out=sine[:, js], in_=rest[:, js], func=ACT.Sin, scale=2.0 * math.pi)

        def put_h2(i, j0, j1, h2):
            nc.vector.tensor_tensor(
                pages[i][:].indirect(entries(idx4, j0, j1)), h2[:], wg2_sb[:, i % PACK, j0:j1], ALU.mult
            )

        def place_h2(i):
            h2 = sbuf("h2_%d" % i, [P, S], F32, tag="h2", bufs=4)
            whole, shift, sine = sine_tiles(i)
            sine_of(i, 0, S, whole, shift, sine, 4 + i % 2)
            if i < ADD_ON_VECTOR:
                nc.vector.tensor_tensor(h2[:], sine[:], bases[i][:], ALU.add)
            else:
                turned = bank("turned%d" % i, 6)
                add_turned(turned, sine, bases[i], 0, S)
                h2_turned = sbuf("h2_turned%d" % i, [P, S], F32, tag="h2_turned", bufs=2)
                nc.scalar.copy(out=h2_turned[:], in_=turned[:])
                back = bank("back%d" % i, 7)
                for c in range(CHUNKS):
                    js = slice(c * P, (c + 1) * P)
                    nc.tensor.transpose(back[:, js], h2_turned[:, js], ident[:])
                nc.scalar.copy(out=h2[:], in_=back[:])
            put_h2(i, 0, S, h2)

        v2_codes, v2_plane = pick_table("v2", tab2_sb, tab2_sc, idx2, 2)

        w2_codes = sbuf("w2_codes", [P, HALVES, 2 * H], U8)
        w2_plane = sbuf("w2_plane", [P, HALVES, H], U8)
        nc.vector.tensor_copy(
            w2_codes[:].bitcast(U16).rearrange("p a (b t q) -> p (a b) t q", b=HALVES, t=PACK),
            w2_sb[:].bitcast(U16).rearrange("p a (b q t) -> p (a b) t q", b=HALVES, t=PACK),
        )
        nc.vector.tensor_copy(
            w2_plane[:].rearrange("p a (b t q) -> p (a b) t q", b=HALVES, t=PACK),
            w2_sc[:].rearrange("p a (b q t) -> p (a b) t q", b=HALVES, t=PACK),
        )

        first_tiles = sine_tiles(0)
        for piece in range(2):
            j0, j1 = piece * S // 2, (piece + 1) * S // 2
            h2_piece = sbuf("h2_piece%d" % piece, [P, S // 2], F32, tag="h2_piece")
            for c in range(j0 // P, j1 // P):
                turns_of_chunk(0, c, 4 + c)
            sine_of(0, j0, j1, *first_tiles, 4 + piece)
            nc.vector.tensor_tensor(h2_piece[:], first_tiles[2][:, j0:j1], bases[0][:, j0:j1], ALU.add)
            put_h2(0, j0, j1, h2_piece)

        gx_sign = sbuf("gx_sign", [P, HALVES, PACK], F32)
        nc.vector.tensor_scalar(gx_sign[:], gx_sb[:], 0.0, 2.0, ALU.is_ge, ALU.mult)
        nc.vector.tensor_scalar(gx_sign[:], gx_sign[:], 1.0, -1.0, ALU.mult, ALU.add)
        v_codes, v_plane = pick_table("v", tab_sb, tab_sc, idx, 1)
        place_h2(1)

        w1_q, t_q = [], []
        for b in range(HALVES):
            w1_woven = woven("w1_woven%d" % b)
            nc.scalar.copy(
                out=w1_woven[:].rearrange("p (t m j) -> p m t j", t=PACK, j=PACK),
                in_=w1_rows[b][:].rearrange("p j (m t) -> p m t j", t=PACK),
            )
            w1_q.append(quantize_pass("w1_%d" % b, w1_woven))
            if b == 1:
                for c in range(CHUNKS):
                    turns_of_chunk(1, c, 6 + c % 2)
            place_h2(2 + 2 * b)
            tanh_y = sbuf("tanh_y%d" % b, [P, S, PACK], F32, tag="stage%d" % (2 * b))
            for c in range(CHUNKS):
                y = bank("y%d_%d" % (b, c), c)
                js = slice(c * P, (c + 1) * P)
                for t in range(PACK):
                    ms = slice(t * P, (t + 1) * P)
                    mx(y[:, ms], w1_q[b][0][:, ms], w1_q[b][1][:, ms], v_codes[:, js], v_plane[:, js], True, True)
                nc.scalar.activation(out=tanh_y[:, js, :], in_=y[:].rearrange("p (t j) -> p j t", t=PACK), func=ACT.Tanh)
            t_woven = woven("t_woven%d" % b)
            nc.vector.tensor_tensor(
                t_woven[:].rearrange("p (j t) -> p j t", t=PACK),
                tanh_y[:], gt_sb[:, b : b + 1, :].to_broadcast([P, S, PACK]), ALU.mult,
            )
            t_q.append(quantize_pass("t_%d" % b, t_woven))
            place_h2(3 + 2 * b)
        h2_placed = 2 + 2 * HALVES

        def place_h1(i):
            w1_codes, w1_plane = w1_q[i // PACK]
            ms = slice((i % PACK) * P, (i % PACK + 1) * P)
            acc = bank("h1_acc%d" % i, i % PACK)
            for a in reversed(range(HALVES)):
                mx(
                    acc[:], w2_codes[:, a, 2 * P * i : 2 * P * (i + 1)], w2_plane[:, a, P * i : P * (i + 1)],
                    t_q[a][0][:], t_q[a][1][:], a == HALVES - 1, False, lhs_dtype=FP4X4,
                )
            mx(acc[:], w1_codes[:, ms], w1_plane[:, ms], v_codes[:], v_plane[:], False, True)
            h1 = sbuf("h1_%d" % i, [P, S], F32, tag="h1", bufs=4)
            nc.scalar.copy(out=h1[:], in_=acc[:])
            nc.vector.tensor_tensor(pages[i][:].indirect(idx3[:]), h1[:], wg1_sb[:, i % PACK, :], ALU.mult)

        x_rows = [sbuf("x_rows%d" % b, [P, PACK, PN], BF16, tag="wide%d" % b) for b in range(HALVES)]
        x_codes = [sbuf("x_codes%d" % b, [P, PN], U32, tag="codes", bufs=2) for b in range(HALVES)]
        x_plane = [sbuf("x_plane%d" % b, [P, PN], U8) for b in range(HALVES)]
        x_last_woven = sbuf("x_last_woven", [P, PN, PACK], BF16, tag="stage2")

        def read_slots(i, j0, j1, tag, bufs):
            picked = sbuf("picked%d_%d" % (i, j0), [P, j1 - j0], F32, tag=tag, bufs=bufs)
            nc.vector.tensor_copy(picked[:], pages[i][:].indirect(entries(idx5, j0, j1)))
            return picked

        def gain_slots(i, j0, j1, picked):
            b, t = i // PACK, i % PACK
            nc.scalar.activation(out=x_rows[b][:, t, j0:j1], in_=picked[:], func=ACT.Abs, scale=gx_sb[:, b, t : t + 1])

        def quantize_first_x():
            for j in range(0, PN, HALF):
                x_woven = woven("x_woven%d" % j)
                nc.scalar.copy(
                    out=x_woven[:].rearrange("p (c i t) -> p c t i", i=RUN, t=PACK),
                    in_=x_rows[0][:, :, j : j + HALF].rearrange("p t (c i) -> p c t i", i=RUN),
                )
                quantize(x_codes[0][:, j : j + HALF], x_plane[0][:, j : j + HALF], x_woven[:])

        def weave_pair(copy, t0, j0, j1):
            copy(x_last_woven[:, j0:j1, t0 : t0 + 2], x_rows[1][:, t0 : t0 + 2, j0:j1].rearrange("p t j -> p j t"))

        def quantize_wo(b):
            wo_signed = woven("wo_signed%d" % b)
            for t in range(PACK):
                nc.scalar.activation(
                    out=wo_signed[:, t * N : (t + 1) * N], in_=wo_rows[b][:, t, :], func=ACT.Copy,
                    scale=gx_sign[:, b, t : t + 1],
                )
            wo_woven = woven("wo_woven%d" % b)
            nc.scalar.copy(
                out=wo_woven[:].rearrange("p (c i t) -> p c t i", i=RUN, t=PACK),
                in_=wo_signed[:].rearrange("p (t c i) -> p c t i", i=RUN, t=PACK),
            )
            return quantize_pass("wo_%d" % b, wo_woven)

        picks = []
        for i in range(AHEAD):
            place_h1(i)
            picks.append(read_slots(i, 0, PN, "picked", 4))
        wo_q = [quantize_wo(0)]
        for i in range(LAST):
            if h2_placed + i < TILES:
                place_h2(h2_placed + i)
            if i + AHEAD < TILES:
                place_h1(i + AHEAD)
            if i + AHEAD < LAST:
                picks.append(read_slots(i + AHEAD, 0, PN, "picked", 4))
            gain_slots(i, 0, PN, picks[i])
            if i == 0:
                wo_q.append(quantize_wo(1))
            if i == PACK - 1:
                quantize_first_x()
            if i == PACK + 1:
                weave_pair(nc.scalar.copy, 0, 0, PN)

        def score_pass(acc, b, pair, q):
            wo_codes, wo_plane = wo_q[b]
            js = slice(q * QUARTER, (q + 1) * QUARTER)
            for side in range(2):
                ns = slice((2 * pair + side) * P, (2 * pair + side + 1) * P)
                mx(
                    acc[:, side * QUARTER : (side + 1) * QUARTER], wo_codes[:, ns], wo_plane[:, ns],
                    x_codes[b][:, js], x_plane[b][:, js], b == 0 and side == 0, b == 1 and side == 1,
                )

        scores = {}
        for q in range(QUARTERS):
            for pair in range(2):
                scores[q, pair] = bank("score%d_%d" % (q, pair), (4 + 2 * q + pair) % 8)
                score_pass(scores[q, pair], 0, pair, q)

        def finish(q):
            for pair in range(2):
                score_pass(scores[q, pair], 1, pair, q)
                result = sbuf("result%d_%d" % (q, pair), [P, 2, QUARTER], F32, tag="page%d" % (2 * q + pair))
                nc.scalar.activation(
                    out=result[:].rearrange("p u j -> p (u j)"), in_=scores[q, pair][:], func=ACT.Tanh
                )
                rows = out[2 * pair * P : 2 * (pair + 1) * P, q * QUARTER : (q + 1) * QUARTER]
                nc.sync.dma_start(rows.rearrange("(u p) j -> p u j", u=2), result[:])

        parts = [read_slots(LAST, q * QUARTER, (q + 1) * QUARTER, "sine", 2) for q in range(2)]
        gain_slots(LAST, 0, QUARTER, parts[0])
        for q in range(QUARTERS):
            j0, j1 = q * QUARTER, (q + 1) * QUARTER
            if q + 1 < QUARTERS:
                gain_slots(LAST, j1, j1 + QUARTER, parts[q + 1])
            weave_pair(nc.vector.tensor_copy, 2, j0, j1)
            quantize(x_codes[1][:, j0:j1], x_plane[1][:, j0:j1], x_last_woven[:, j0:j1, :].rearrange("p j t -> p (j t)"))
            if q + 2 < QUARTERS:
                parts.append(read_slots(LAST, j0 + 2 * QUARTER, j1 + 2 * QUARTER, "sine", 2))
            if q >= 1:
                finish(q - 1)
        finish(QUARTERS - 1)
